import numpy as np
import ml_dtypes


def mxq(x, axis, fmt="e4m3"):
    dtype, down = {"e4m3": (ml_dtypes.float8_e4m3fn, 7), "e5m2": (ml_dtypes.float8_e5m2, 14)}[fmt]
    v = np.moveaxis(np.asarray(x, np.float32).astype(ml_dtypes.bfloat16).astype(np.float64), axis, -1)
    blocks = v.reshape(v.shape[:-1] + (-1, 32))
    amax = np.abs(blocks).max(-1, keepdims=True)
    byte = np.maximum(np.where(amax > 0, np.frexp(amax)[1] - 1 + 127, 0) - down, 1)
    scale = np.exp2(byte - 127.0)
    codes = (blocks / scale).astype(np.float32).astype(dtype).astype(np.float64)
    return np.moveaxis((codes * scale).reshape(v.shape), -1, axis)


WIDE = False


def mx_kscale(k):
    if not WIDE:
        return np.ones(k)
    levels = np.array([10, -10, 5, -5, 0])
    if k % 512:
        return np.exp2(np.random.permutation(np.resize(levels, k // 32))).repeat(32)
    a = np.empty((k // 512, 16))
    for p in range(k // 512):
        a[p, :8] = np.random.permutation(np.resize(levels, 8))
        for g in range(8):
            far = levels[np.abs(levels - a[p, g]) >= 10]
            a[p, g + 8] = far[np.random.randint(len(far))]
    return np.exp2(a.ravel()).repeat(32)


BF16 = ml_dtypes.bfloat16


def bf(x):
    return np.asarray(x, np.float32).astype(BF16)


def f64(x):
    return np.asarray(x).astype(np.float64)

def planes(Y):
    n, m = Y.shape
    b = f64(bf(Y)).reshape(n // 32, 32, m)
    amax = np.abs(b).max(1)
    byte = np.clip(np.where(amax > 0, np.frexp(amax)[1] - 1 + 127 - 7, 1), 1, 254)
    codes = (b * np.exp2(127.0 - byte)[:, None, :]).reshape(n, m).astype(np.float32).astype(ml_dtypes.float8_e4m3fn).view(np.uint8)
    words = codes.reshape(n // 512, 128, 4, m).transpose(0, 1, 3, 2)
    return np.ascontiguousarray(words), np.ascontiguousarray(byte.astype(np.uint8).reshape(n // 512, 16, m))


B, T, C, F, R = 8, 1024, 512, 512, 128

def setup_inputs():
    s = mx_kscale(C)
    t = mx_kscale(T)
    time = np.arange(T) / T
    envelope = np.exp(0.6 * np.sin(2 * np.pi * (time[None, :, None] + np.random.rand(B, 1, 1))))
    size = np.exp(0.3 * np.random.randn(B, 1, C))
    x = np.random.randn(B, T, C) * envelope * size
    filters = np.random.randn(C, F) / np.sqrt(C) * np.exp(0.4 * np.random.randn(F))
    sample_weights = np.exp(0.5 * np.random.randn(T))
    latency = np.random.rand(R, 1)
    sharpness = 0.5 + 1.5 * np.random.rand(R, 1)
    averaging = np.exp(sharpness * np.cos(2 * np.pi * (time[None, :] - latency)) + 0.3 * np.random.randn(R, T))
    averaging = averaging / averaging.sum(axis=1, keepdims=True)
    return {
        "x": bf(x * s),
        "filters": bf(filters / s[:, None]),
        "sample_weights": bf(sample_weights * t),
        "averaging": bf(averaging / t),
        "power_offset": bf(0.2 * np.exp(0.3 * np.random.randn(F))),
        "gain": bf(np.exp(0.8 * np.random.randn(F))),
        "bias": bf(0.3 * np.random.randn(F)),
    }

def reference(x, filters, sample_weights, averaging, power_offset, gain, bias):
    S = mxq(f64(x), 2, "e4m3") @ mxq(f64(filters), 0, "e4m3")
    P = S * S * f64(sample_weights)[:, None]
    L = mxq(f64(averaging), 1, "e4m3") @ mxq(P, 1, "e4m3")
    y = np.log(L + f64(power_offset)) * f64(gain) + f64(bias)
    Y = y.reshape(B * R, F).T
    words, scales = planes(Y)
    return y, words, scales

@@ -1,0 +1,338 @@
+from contextlib import ExitStack
+
+import concourse.mybir as mybir
+from concourse.masks import make_identity
+
+B, T, C, F, R = 8, 1024, 512, 512, 128
+FLOPS = 2 * B * T * C * F + 2 * B * R * T * F
+
+F32 = mybir.dt.float32
+BF16 = mybir.dt.bfloat16
+I32 = mybir.dt.int32
+U32 = mybir.dt.uint32
+U8 = mybir.dt.uint8
+FP8X4 = mybir.dt.float8_e4m3fn_x4
+ALU = mybir.AluOpType
+ACT = mybir.ActivationFunctionType
+
+P = 128
+PACK = 4
+SPAN = P * PACK
+HALVES = T // SPAN
+UNITS = B * HALVES
+SQRT_FLOOR = 2.0 ** -116
+
+
+def interleave_views(dst, src):
+    return (
+        dst.rearrange("p (c i t) -> p c t i", i=4, t=PACK),
+        src.rearrange("p t (c i) -> p c t i", i=4),
+    )
+
+
+def tile_motor_imagery_log_power_h3_kernel(
+    tc, x, filters, sample_weights, averaging, power_offset, gain, bias, out_0, out_1, out_2
+):
+    nc = tc.nc
+    with ExitStack() as ctx:
+        keep = ctx.enter_context(tc.tile_pool(name="keep", bufs=1))
+        work = ctx.enter_context(tc.tile_pool(name="work", bufs=3))
+        psum = ctx.enter_context(tc.psum_pool(name="psum", bufs=1))
+        ctx.enter_context(tc.manual_schedule())
+
+        x_rows = x.rearrange("b (g p j) c -> (b g) p j c", g=HALVES, j=PACK)
+        x_raw = {}
+
+        def load_x(u, h):
+            x_raw[u, h] = keep.tile([P, 2 * C], BF16, name="x_raw_%d_%d" % (u, h))
+            nc.sync.dma_start(
+                out=x_raw[u, h][:].rearrange("p (j c) -> p j c", j=2), in_=x_rows[u, :, 2 * h : 2 * h + 2, :]
+            )
+
+        w_raw = keep.tile([P, HALVES, 16], BF16)
+        nc.sync.dma_start(out=w_raw[:, :, 0:PACK], in_=sample_weights.rearrange("(g p j) -> p g j", g=HALVES, j=PACK))
+        load_x(0, 0)
+        f_raw = keep.tile([P, PACK, F], BF16)
+        nc.sync.dma_start(out=f_raw[:], in_=filters.rearrange("(p j) f -> p j f", j=PACK))
+        load_x(0, 1)
+        load_x(1, 0)
+        load_x(1, 1)
+        a_raw = keep.tile([P, T], BF16)
+        nc.sync.dma_start(out=a_raw[:], in_=averaging)
+        load_x(2, 0)
+        load_x(2, 1)
+        offset_col = keep.tile([P, PACK], BF16)
+        gain_col = keep.tile([P, PACK], BF16)
+        bias_col = keep.tile([P, PACK], BF16)
+        for col, vec in ((offset_col, power_offset), (gain_col, gain), (bias_col, bias)):
+            nc.sync.dma_start(out=col[:], in_=vec.rearrange("(p s) -> p s", s=PACK))
+        for u in range(3, UNITS):
+            load_x(u, 0)
+            load_x(u, 1)
+
+        ident = keep.tile([P, P], F32)
+        make_identity(nc, ident[:])
+        one = keep.tile([P, 1], F32)
+        nc.vector.memset(one[:], 1.0)
+
+        w = w_raw[:, :, 0:PACK]
+        w_neg = keep.tile([P, HALVES, PACK], F32)
+        w_abs = keep.tile([P, HALVES, PACK], F32)
+        root0 = keep.tile([P, HALVES, PACK], F32)
+        root_inv = keep.tile([P, HALVES, PACK], F32)
+        half_quot = keep.tile([P, HALVES, PACK], F32)
+        root = keep.tile([P, HALVES, PACK], F32)
+        w_ge = keep.tile([P, HALVES, PACK], F32)
+        w_sign = keep.tile([P, HALVES, PACK], BF16)
+        warm = keep.tile([P, 1], F32)
+        nc.vector.tensor_scalar(out=w_neg[:], in0=w, scalar1=-1.0, scalar2=SQRT_FLOOR, op0=ALU.mult, op1=ALU.max)
+        nc.vector.tensor_tensor(out=w_abs[:], in0=w_neg[:], in1=w, op=ALU.max)
+        nc.scalar.activation(out=root0[:], in_=w_abs[:], func=ACT.Sqrt)
+        nc.scalar.activation(out=warm[:], in_=one[:], func=ACT.Ln)
+        nc.vector.tensor_scalar(out=w_ge[:], in0=w, scalar1=0.0, scalar2=2.0, op0=ALU.is_ge, op1=ALU.mult)
+        nc.vector.tensor_scalar(out=w_sign[:], in0=w_ge[:], scalar1=-1.0, scalar2=None, op0=ALU.add)
+        nc.vector.reciprocal(out=root_inv[:], in_=root0[:])
+        nc.vector.scalar_tensor_tensor(
+            out=half_quot[:], in0=w_abs[:], scalar=0.5, in1=root_inv[:], op0=ALU.mult, op1=ALU.mult
+        )
+        nc.vector.scalar_tensor_tensor(
+            out=root[:], in0=root0[:], scalar=0.5, in1=half_quot[:], op0=ALU.mult, op1=ALU.add
+        )
+
+        def quantize(codes, scales, grouped):
+            nc.vector.quantize_mx(out=codes.bitcast(FP8X4), scales=scales, in_=grouped)
+
+        x_bank, x_grouped, x_codes, x_scales = {}, {}, {}, {}
+        s_bank, p_rows, p_grouped, p_codes, p_scales = {}, {}, {}, {}, {}
+        l_bank, log_power, y_rows, y_grouped, y_bank = {}, {}, {}, {}, {}
+        f_codes = keep.tile([P, F], U32, align_bytes=64)
+        f_scales = keep.tile([P, F], U8, align_bytes=64)
+        a_codes = keep.tile([P, HALVES * R], U32, align_bytes=64)
+        a_scales = keep.tile([P, HALVES * R], U8, align_bytes=64)
+        y_codes = keep.tile([P, B * R], U32, align_bytes=64)
+        y_scales = keep.tile([P, B * R], U8, align_bytes=64)
+
+        def turn_x(u, h):
+            if not 0 <= u < UNITS:
+                return
+            x_bank[u, h] = psum.tile([P, 2, 2, P], F32, name="x_bank", tag="x_bank_%d" % h)
+            words = x_raw[u, h][:].bitcast(F32)
+            for j in range(2):
+                for e in range(2):
+                    nc.tensor.transpose(
+                        x_bank[u, h][:, j, e, :], words[:, 256 * j + e : 256 * (j + 1) : 2], ident[:]
+                    )
+
+        def copy_x(u, h, on_scalar):
+            if not 0 <= u < UNITS:
+                return
+            x_grouped[u, h] = work.tile([P, 2 * SPAN], BF16, name="x_grouped", tag="x_grouped_%d" % h, align_bytes=64)
+            dst = x_grouped[u, h][:].bitcast(F32).rearrange("p (j m e) -> p j m e", j=2, e=2)
+            src = x_bank[u, h][:].rearrange("p j e m -> p j m e")
+            if on_scalar:
+                nc.scalar.copy(out=dst, in_=src)
+            else:
+                nc.vector.tensor_copy(out=dst, in_=src)
+
+        def quantize_x(u, h):
+            if not 0 <= u < UNITS:
+                return
+            x_codes[u, h] = work.tile([P, 2 * P], U32, name="x_codes", tag="x_codes_%d" % h, align_bytes=64)
+            x_scales[u, h] = work.tile([P, 2 * P], U8, name="x_scales", tag="x_scales_%d" % h, align_bytes=64)
+            quantize(x_codes[u, h][:], x_scales[u, h][:], x_grouped[u, h][:])
+
+        def filter_pass(u, j):
+            if not 0 <= u < UNITS:
+                return
+            s_bank[u, j] = psum.tile([P, F], F32, name="s_bank", tag="s_bank_%d" % j)
+            cols = slice(P * (j % 2), P * (j % 2 + 1))
+            nc.tensor.matmul_mx(
+                out=s_bank[u, j][:],
+                lhsT=x_codes[u, j // 2][:, cols].bitcast(FP8X4),
+                lhsT_scale=x_scales[u, j // 2][:, cols],
+                rhs=f_codes[:].bitcast(FP8X4),
+                rhs_scale=f_scales[:],
+                start=True,
+                stop=True,
+            )
+
+        def square(u, j):
+            if not 0 <= u < UNITS:
+                return
+            if j == 0:
+                p_rows[u] = work.tile([P, PACK, F], BF16, name="p_rows", tag="p_rows")
+            nc.scalar.activation(
+                out=p_rows[u][:, j, :], in_=s_bank[u, j][:], func=ACT.Square, scale=root[:, u % HALVES, j : j + 1]
+            )
+
+        def interleave_p(u):
+            if not 0 <= u < UNITS:
+                return
+            p_grouped[u] = work.tile([P, PACK * F], BF16, name="p_grouped", tag="p_grouped", align_bytes=64)
+            dst, src = interleave_views(p_grouped[u][:], p_rows[u][:])
+            nc.vector.tensor_copy(out=dst, in_=src)
+
+        def quantize_p(u):
+            if not 0 <= u < UNITS:
+                return
+            p_codes[u] = work.tile([P, F], U32, name="p_codes", tag="p_codes", align_bytes=64)
+            p_scales[u] = work.tile([P, F], U8, name="p_scales", tag="p_scales", align_bytes=64)
+            quantize(p_codes[u][:], p_scales[u][:], p_grouped[u][:])
+
+        def average(i):
+            if not 0 <= i < B:
+                return
+            l_bank[i] = psum.tile([P, PACK, R], F32, name="l_bank", tag="l_bank")
+            for s in range(PACK):
+                cols = slice(P * s, P * (s + 1))
+                for g in range(HALVES):
+                    windows = slice(R * g, R * (g + 1))
+                    nc.tensor.matmul_mx(
+                        out=l_bank[i][:, s, :],
+                        lhsT=p_codes[HALVES * i + g][:, cols].bitcast(FP8X4),
+                        lhsT_scale=p_scales[HALVES * i + g][:, cols],
+                        rhs=a_codes[:, windows].bitcast(FP8X4),
+                        rhs_scale=a_scales[:, windows],
+                        start=(g == 0),
+                        stop=(g == HALVES - 1),
+                    )
+
+        def take_log(i, slots):
+            if not 0 <= i < B:
+                return
+            if slots[0] == 0:
+                log_power[i] = work.tile([P, PACK, R], F32, name="log_power", tag="log_power")
+            for s in slots:
+                nc.scalar.activation(
+                    out=log_power[i][:, s, :], in_=l_bank[i][:, s, :], func=ACT.Ln, bias=offset_col[:, s : s + 1]
+                )
+
+        def gain_and_bias(i):
+            if not 0 <= i < B:
+                return
+            y_rows[i] = work.tile([P, PACK, R], F32, name="y_rows", tag="y_rows")
+            for s in range(PACK):
+                nc.vector.tensor_scalar(
+                    out=y_rows[i][:, s, :],
+                    in0=log_power[i][:, s, :],
+                    scalar1=gain_col[:, s : s + 1],
+                    scalar2=bias_col[:, s : s + 1],
+                    op0=ALU.mult,
+                    op1=ALU.add,
+                )
+
+        def round_y(i):
+            if not 0 <= i < B:
+                return
+            y_grouped[i] = work.tile([P, PACK * R], BF16, name="y_grouped", tag="y_grouped", align_bytes=64)
+            dst, src = interleave_views(y_grouped[i][:], y_rows[i][:])
+            nc.vector.tensor_copy(out=dst, in_=src)
+
+        def quantize_y(i):
+            if not 0 <= i < B:
+                return
+            cols = slice(R * i, R * (i + 1))
+            quantize(y_codes[:, cols], y_scales[:, cols], y_grouped[i][:])
+            nc.sync.dma_start(
+                out=out_1[0].rearrange("p m t -> p (m t)").bitcast(I32)[:, cols], in_=y_codes[:, cols].bitcast(I32)
+            )
+            if i == B - 1:
+                for q in range(4):
+                    nc.sync.dma_start(
+                        out=out_2[0, 4 * q : 4 * q + 4, :].bitcast(I32),
+                        in_=y_scales[32 * q : 32 * q + 4, :].bitcast(I32),
+                    )
+
+        def turn_y(i):
+            if not 0 <= i < B:
+                return
+            y_bank[i] = psum.tile([P, PACK, P], F32, name="y_bank", tag="y_bank")
+            for s in range(PACK):
+                nc.tensor.transpose(y_bank[i][:, s, :], y_rows[i][:, s, :], ident[:])
+
+        def store_y(i):
+            if not 0 <= i < B:
+                return
+            y_out = work.tile([P, F], F32, name="y_out", tag="y_out")
+            dst = y_out[:].rearrange("r (p s) -> r p s", s=PACK)
+            src = y_bank[i][:].rearrange("r s p -> r p s")
+            if i in (B - 3, B - 2):
+                nc.vector.tensor_copy(out=dst, in_=src)
+            else:
+                nc.scalar.copy(out=dst, in_=src)
+            nc.sync.dma_start(out=out_0[i], in_=y_out[:])
+
+        turn_x(0, 0)
+        turn_x(0, 1)
+        f_grouped = keep.tile([P, PACK * F], BF16, align_bytes=64)
+        nc.vector.tensor_copy(
+            out=f_grouped[:].rearrange("p (s m j) -> p m s j", s=PACK, j=PACK),
+            in_=f_raw[:].rearrange("p j (m s) -> p m s j", s=PACK),
+        )
+        copy_x(0, 0, True)
+        copy_x(0, 1, True)
+        quantize_x(0, 0)
+        quantize(f_codes[:], f_scales[:], f_grouped[:])
+        quantize_x(0, 1)
+        turn_x(1, 0)
+        filter_pass(0, 0)
+        filter_pass(0, 1)
+        copy_x(1, 0, True)
+        turn_x(1, 1)
+        filter_pass(0, 2)
+        filter_pass(0, 3)
+        copy_x(1, 1, False)
+
+        a_bank = psum.tile([P, HALVES, 2, R], F32, name="a_bank", tag="y_bank")
+        a_words = a_raw[:].bitcast(F32)
+        for g in range(HALVES):
+            for e in range(2):
+                nc.tensor.transpose(a_bank[:, g, e, :], a_words[:, 256 * g + e : 256 * (g + 1) : 2], ident[:])
+        a_turned = keep.tile([P, T], BF16, align_bytes=64)
+        a_signed = keep.tile([P, T], BF16, align_bytes=64)
+        nc.vector.tensor_copy(
+            out=a_turned[:].bitcast(F32).rearrange("p (g r e) -> p g r e", g=HALVES, e=2),
+            in_=a_bank[:].rearrange("p g e r -> p g r e"),
+        )
+
+        def sign_averaging():
+            nc.vector.tensor_tensor(
+                out=a_signed[:].rearrange("p (g r j) -> p g r j", g=HALVES, j=PACK),
+                in0=a_turned[:].rearrange("p (g r j) -> p g r j", g=HALVES, j=PACK),
+                in1=w_sign[:].unsqueeze(2).to_broadcast([P, HALVES, R, PACK]),
+                op=ALU.mult,
+            )
+
+        for u in range(UNITS + 3):
+            odd = u % 2 == 1
+            early = (u - 2) // 2 if not odd else -1
+            middle = (u - 3) // 2 if odd else -1
+            late = (u - 4) // 2 if not odd else -1
+            quantize_x(u + 1, 0)
+            square(u, 0)
+            filter_pass(u + 1, 0)
+            if u == 0:
+                sign_averaging()
+            interleave_p(u - 1)
+            turn_x(u + 2, 0)
+            take_log(middle, (0, 1))
+            square(u, 1)
+            filter_pass(u + 1, 1)
+            turn_x(u + 2, 1)
+            quantize_x(u + 1, 1)
+            round_y(late)
+            take_log(middle, (2, 3))
+            store_y(late)
+            if u == 0:
+                quantize(a_codes[:], a_scales[:], a_signed[:])
+            quantize_p(u - 1)
+            square(u, 2)
+            filter_pass(u + 1, 2)
+            average(early)
+            gain_and_bias(middle)
+            quantize_y(late)
+            copy_x(u + 2, 0, True)
+            square(u, 3)
+            filter_pass(u + 1, 3)
+            turn_y(middle)
+            copy_x(u + 2, 1, False)

@@ -52,21 +52,27 @@ def tile_motor_imagery_log_power_h3_kernel(
         w_raw = keep.tile([P, HALVES, 16], BF16)
         nc.sync.dma_start(out=w_raw[:, :, 0:PACK], in_=sample_weights.rearrange("(g p j) -> p g j", g=HALVES, j=PACK))
         load_x(0, 0)
-        f_raw = keep.tile([P, PACK, F], BF16)
-        nc.sync.dma_start(out=f_raw[:], in_=filters.rearrange("(p j) f -> p j f", j=PACK))
+        f_raw = {}
+        for h in range(2):
+            f_raw[h] = keep.tile([P, PACK, F // 2], BF16, name="f_raw_%d" % h)
+            nc.sync.dma_start(
+                out=f_raw[h][:], in_=filters.rearrange("(p j) f -> p j f", j=PACK)[:, :, h * F // 2 : (h + 1) * F // 2]
+            )
         load_x(0, 1)
         load_x(1, 0)
         load_x(1, 1)
-        a_raw = keep.tile([P, T], BF16)
-        nc.sync.dma_start(out=a_raw[:], in_=averaging)
         load_x(2, 0)
         load_x(2, 1)
+        a_raw = keep.tile([P, T], BF16)
+        nc.sync.dma_start(out=a_raw[:], in_=averaging)
+        load_x(3, 0)
+        load_x(3, 1)
         offset_col = keep.tile([P, PACK], BF16)
         gain_col = keep.tile([P, PACK], BF16)
         bias_col = keep.tile([P, PACK], BF16)
         for col, vec in ((offset_col, power_offset), (gain_col, gain), (bias_col, bias)):
             nc.sync.dma_start(out=col[:], in_=vec.rearrange("(p s) -> p s", s=PACK))
-        for u in range(3, UNITS):
+        for u in range(4, UNITS):
             load_x(u, 0)
             load_x(u, 1)
 
@@ -76,28 +82,21 @@ def tile_motor_imagery_log_power_h3_kernel(
         nc.vector.memset(one[:], 1.0)
 
         w = w_raw[:, :, 0:PACK]
-        w_neg = keep.tile([P, HALVES, PACK], F32)
         w_abs = keep.tile([P, HALVES, PACK], F32)
         root0 = keep.tile([P, HALVES, PACK], F32)
         root_inv = keep.tile([P, HALVES, PACK], F32)
         half_quot = keep.tile([P, HALVES, PACK], F32)
         root = keep.tile([P, HALVES, PACK], F32)
+        w_neg = keep.tile([P, HALVES, PACK], F32)
         w_ge = keep.tile([P, HALVES, PACK], F32)
         w_sign = keep.tile([P, HALVES, PACK], BF16)
         warm = keep.tile([P, 1], F32)
         nc.vector.tensor_scalar(out=w_neg[:], in0=w, scalar1=-1.0, scalar2=SQRT_FLOOR, op0=ALU.mult, op1=ALU.max)
+        nc.vector.tensor_scalar(out=w_ge[:], in0=w, scalar1=0.0, scalar2=2.0, op0=ALU.is_ge, op1=ALU.mult)
         nc.vector.tensor_tensor(out=w_abs[:], in0=w_neg[:], in1=w, op=ALU.max)
+        nc.vector.tensor_scalar(out=w_sign[:], in0=w_ge[:], scalar1=-1.0, scalar2=None, op0=ALU.add)
         nc.scalar.activation(out=root0[:], in_=w_abs[:], func=ACT.Sqrt)
         nc.scalar.activation(out=warm[:], in_=one[:], func=ACT.Ln)
-        nc.vector.tensor_scalar(out=w_ge[:], in0=w, scalar1=0.0, scalar2=2.0, op0=ALU.is_ge, op1=ALU.mult)
-        nc.vector.tensor_scalar(out=w_sign[:], in0=w_ge[:], scalar1=-1.0, scalar2=None, op0=ALU.add)
-        nc.vector.reciprocal(out=root_inv[:], in_=root0[:])
-        nc.vector.scalar_tensor_tensor(
-            out=half_quot[:], in0=w_abs[:], scalar=0.5, in1=root_inv[:], op0=ALU.mult, op1=ALU.mult
-        )
-        nc.vector.scalar_tensor_tensor(
-            out=root[:], in0=root0[:], scalar=0.5, in1=half_quot[:], op0=ALU.mult, op1=ALU.add
-        )
 
         def quantize(codes, scales, grouped):
             nc.vector.quantize_mx(out=codes.bitcast(FP8X4), scales=scales, in_=grouped)
@@ -112,10 +111,10 @@ def tile_motor_imagery_log_power_h3_kernel(
         y_codes = keep.tile([P, B * R], U32, align_bytes=64)
         y_scales = keep.tile([P, B * R], U8, align_bytes=64)
 
-        def turn_x(u, h):
+        def turn_x(u, h, tag=None):
             if not 0 <= u < UNITS:
                 return
-            x_bank[u, h] = psum.tile([P, 2, 2, P], F32, name="x_bank", tag="x_bank_%d" % h)
+            x_bank[u, h] = psum.tile([P, 2, 2, P], F32, name="x_bank", tag=tag or "x_bank_%d" % h)
             words = x_raw[u, h][:].bitcast(F32)
             for j in range(2):
                 for e in range(2):
@@ -126,69 +125,81 @@ def tile_motor_imagery_log_power_h3_kernel(
         def copy_x(u, h, on_scalar):
             if not 0 <= u < UNITS:
                 return
-            x_grouped[u, h] = work.tile([P, 2 * SPAN], BF16, name="x_grouped", tag="x_grouped_%d" % h, align_bytes=64)
-            dst = x_grouped[u, h][:].bitcast(F32).rearrange("p (j m e) -> p j m e", j=2, e=2)
+            if u not in x_grouped:
+                x_grouped[u] = work.tile([P, PACK * SPAN], BF16, name="x_grouped", tag="x_grouped", align_bytes=64)
+            dst = x_grouped[u][:, 2 * SPAN * h : 2 * SPAN * (h + 1)].bitcast(F32)
+            dst = dst.rearrange("p (j m e) -> p j m e", j=2, e=2)
             src = x_bank[u, h][:].rearrange("p j e m -> p j m e")
             if on_scalar:
                 nc.scalar.copy(out=dst, in_=src)
             else:
                 nc.vector.tensor_copy(out=dst, in_=src)
 
-        def quantize_x(u, h):
+        def quantize_x(u, j0=0, j1=PACK):
             if not 0 <= u < UNITS:
                 return
-            x_codes[u, h] = work.tile([P, 2 * P], U32, name="x_codes", tag="x_codes_%d" % h, align_bytes=64)
-            x_scales[u, h] = work.tile([P, 2 * P], U8, name="x_scales", tag="x_scales_%d" % h, align_bytes=64)
-            quantize(x_codes[u, h][:], x_scales[u, h][:], x_grouped[u, h][:])
+            if j0 == 0:
+                x_codes[u] = work.tile([P, SPAN], U32, name="x_codes", tag="x_codes", align_bytes=64)
+                x_scales[u] = work.tile([P, SPAN], U8, name="x_scales", tag="x_scales", align_bytes=64)
+            cols = slice(P * j0, P * j1)
+            quantize(x_codes[u][:, cols], x_scales[u][:, cols], x_grouped[u][:, SPAN * j0 : SPAN * j1])
 
         def filter_pass(u, j):
             if not 0 <= u < UNITS:
                 return
             s_bank[u, j] = psum.tile([P, F], F32, name="s_bank", tag="s_bank_%d" % j)
-            cols = slice(P * (j % 2), P * (j % 2 + 1))
+            cols = slice(P * j, P * (j + 1))
             nc.tensor.matmul_mx(
                 out=s_bank[u, j][:],
-                lhsT=x_codes[u, j // 2][:, cols].bitcast(FP8X4),
-                lhsT_scale=x_scales[u, j // 2][:, cols],
+                lhsT=x_codes[u][:, cols].bitcast(FP8X4),
+                lhsT_scale=x_scales[u][:, cols],
                 rhs=f_codes[:].bitcast(FP8X4),
                 rhs_scale=f_scales[:],
                 start=True,
                 stop=True,
             )
 
-        def square(u, j):
+        def square(u, j, s0=0, s1=PACK):
             if not 0 <= u < UNITS:
                 return
-            if j == 0:
+            if u not in p_rows:
                 p_rows[u] = work.tile([P, PACK, F], BF16, name="p_rows", tag="p_rows")
+            cols = slice(P * s0, P * s1)
             nc.scalar.activation(
-                out=p_rows[u][:, j, :], in_=s_bank[u, j][:], func=ACT.Square, scale=root[:, u % HALVES, j : j + 1]
+                out=p_rows[u][:, j, cols],
+                in_=s_bank[u, j][:, cols],
+                func=ACT.Square,
+                scale=root[:, u % HALVES, j : j + 1],
             )
 
-        def interleave_p(u):
+        def interleave_p(u, s0=0, s1=PACK):
             if not 0 <= u < UNITS:
                 return
-            p_grouped[u] = work.tile([P, PACK * F], BF16, name="p_grouped", tag="p_grouped", align_bytes=64)
-            dst, src = interleave_views(p_grouped[u][:], p_rows[u][:])
+            if s0 == 0:
+                p_grouped[u] = work.tile([P, PACK * F], BF16, name="p_grouped", tag="p_grouped", align_bytes=64)
+            dst, src = interleave_views(p_grouped[u][:, SPAN * s0 : SPAN * s1], p_rows[u][:, :, P * s0 : P * s1])
             nc.vector.tensor_copy(out=dst, in_=src)
 
-        def quantize_p(u):
+        def quantize_p(u, s0=0, s1=PACK):
             if not 0 <= u < UNITS:
                 return
-            p_codes[u] = work.tile([P, F], U32, name="p_codes", tag="p_codes", align_bytes=64)
-            p_scales[u] = work.tile([P, F], U8, name="p_scales", tag="p_scales", align_bytes=64)
-            quantize(p_codes[u][:], p_scales[u][:], p_grouped[u][:])
+            if s0 == 0:
+                p_codes[u] = work.tile([P, F], U32, name="p_codes", tag="p_codes", bufs=4, align_bytes=64)
+                p_scales[u] = work.tile([P, F], U8, name="p_scales", tag="p_scales", bufs=4, align_bytes=64)
+            cols = slice(P * s0, P * s1)
+            quantize(p_codes[u][:, cols], p_scales[u][:, cols], p_grouped[u][:, SPAN * s0 : SPAN * s1])
 
-        def average(i):
+        def average(i, s0=0, s1=PACK, tag="l_bank"):
             if not 0 <= i < B:
                 return
-            l_bank[i] = psum.tile([P, PACK, R], F32, name="l_bank", tag="l_bank")
-            for s in range(PACK):
+            bank = psum.tile([P, PACK, R], F32, name="l_bank", tag=tag)
+            for s in range(s0, s1):
+                l_bank[i, s] = bank
                 cols = slice(P * s, P * (s + 1))
                 for g in range(HALVES):
                     windows = slice(R * g, R * (g + 1))
                     nc.tensor.matmul_mx(
-                        out=l_bank[i][:, s, :],
+                        out=bank[:, s, :],
                         lhsT=p_codes[HALVES * i + g][:, cols].bitcast(FP8X4),
                         lhsT_scale=p_scales[HALVES * i + g][:, cols],
                         rhs=a_codes[:, windows].bitcast(FP8X4),
@@ -204,14 +215,15 @@ def tile_motor_imagery_log_power_h3_kernel(
                 log_power[i] = work.tile([P, PACK, R], F32, name="log_power", tag="log_power")
             for s in slots:
                 nc.scalar.activation(
-                    out=log_power[i][:, s, :], in_=l_bank[i][:, s, :], func=ACT.Ln, bias=offset_col[:, s : s + 1]
+                    out=log_power[i][:, s, :], in_=l_bank[i, s][:, s, :], func=ACT.Ln, bias=offset_col[:, s : s + 1]
                 )
 
-        def gain_and_bias(i):
+        def gain_and_bias(i, s0=0, s1=PACK):
             if not 0 <= i < B:
                 return
-            y_rows[i] = work.tile([P, PACK, R], F32, name="y_rows", tag="y_rows")
-            for s in range(PACK):
+            if s0 == 0:
+                y_rows[i] = work.tile([P, PACK, R], F32, name="y_rows", tag="y_rows")
+            for s in range(s0, s1):
                 nc.vector.tensor_scalar(
                     out=y_rows[i][:, s, :],
                     in0=log_power[i][:, s, :],
@@ -243,57 +255,51 @@ def tile_motor_imagery_log_power_h3_kernel(
                         in_=y_scales[32 * q : 32 * q + 4, :].bitcast(I32),
                     )
 
-        def turn_y(i):
+        def turn_y(i, s0=0, s1=PACK, tag="y_bank"):
             if not 0 <= i < B:
                 return
-            y_bank[i] = psum.tile([P, PACK, P], F32, name="y_bank", tag="y_bank")
-            for s in range(PACK):
+            if s0 == 0:
+                y_bank[i] = psum.tile([P, PACK, P], F32, name="y_bank", tag=tag)
+            for s in range(s0, s1):
                 nc.tensor.transpose(y_bank[i][:, s, :], y_rows[i][:, s, :], ident[:])
 
-        def store_y(i):
+        def store_y(i, on_scalar=True):
             if not 0 <= i < B:
                 return
             y_out = work.tile([P, F], F32, name="y_out", tag="y_out")
             dst = y_out[:].rearrange("r (p s) -> r p s", s=PACK)
             src = y_bank[i][:].rearrange("r s p -> r p s")
-            if i in (B - 3, B - 2):
-                nc.vector.tensor_copy(out=dst, in_=src)
-            else:
+            if on_scalar:
                 nc.scalar.copy(out=dst, in_=src)
+            else:
+                nc.vector.tensor_copy(out=dst, in_=src)
             nc.sync.dma_start(out=out_0[i], in_=y_out[:])
 
-        turn_x(0, 0)
-        turn_x(0, 1)
         f_grouped = keep.tile([P, PACK * F], BF16, align_bytes=64)
-        nc.vector.tensor_copy(
-            out=f_grouped[:].rearrange("p (s m j) -> p m s j", s=PACK, j=PACK),
-            in_=f_raw[:].rearrange("p j (m s) -> p m s j", s=PACK),
-        )
-        copy_x(0, 0, True)
-        copy_x(0, 1, True)
-        quantize_x(0, 0)
-        quantize(f_codes[:], f_scales[:], f_grouped[:])
-        quantize_x(0, 1)
-        turn_x(1, 0)
-        filter_pass(0, 0)
-        filter_pass(0, 1)
-        copy_x(1, 0, True)
-        turn_x(1, 1)
-        filter_pass(0, 2)
-        filter_pass(0, 3)
-        copy_x(1, 1, False)
-
-        a_bank = psum.tile([P, HALVES, 2, R], F32, name="a_bank", tag="y_bank")
-        a_words = a_raw[:].bitcast(F32)
-        for g in range(HALVES):
-            for e in range(2):
-                nc.tensor.transpose(a_bank[:, g, e, :], a_words[:, 256 * g + e : 256 * (g + 1) : 2], ident[:])
         a_turned = keep.tile([P, T], BF16, align_bytes=64)
         a_signed = keep.tile([P, T], BF16, align_bytes=64)
-        nc.vector.tensor_copy(
-            out=a_turned[:].bitcast(F32).rearrange("p (g r e) -> p g r e", g=HALVES, e=2),
-            in_=a_bank[:].rearrange("p g e r -> p g r e"),
-        )
+
+        def interleave_filters(h):
+            nc.vector.tensor_copy(
+                out=f_grouped[:].rearrange("p (s m j) -> p m s j", s=PACK, j=PACK)[:, 64 * h : 64 * (h + 1)],
+                in_=f_raw[h][:].rearrange("p j (m s) -> p m s j", s=PACK),
+            )
+
+        a_banks = []
+
+        def turn_averaging():
+            a_bank = psum.tile([P, HALVES, 2, R], F32, name="a_bank", tag="y_bank")
+            a_banks.append(a_bank)
+            a_words = a_raw[:].bitcast(F32)
+            for g in range(HALVES):
+                for e in range(2):
+                    nc.tensor.transpose(a_bank[:, g, e, :], a_words[:, 256 * g + e : 256 * (g + 1) : 2], ident[:])
+
+        def copy_averaging():
+            nc.scalar.copy(
+                out=a_turned[:].bitcast(F32).rearrange("p (g r e) -> p g r e", g=HALVES, e=2),
+                in_=a_banks[0][:].rearrange("p g e r -> p g r e"),
+            )
 
         def sign_averaging():
             nc.vector.tensor_tensor(
@@ -303,36 +309,148 @@ def tile_motor_imagery_log_power_h3_kernel(
                 op=ALU.mult,
             )
 
-        for u in range(UNITS + 3):
+        turn_x(0, 0)
+        interleave_filters(0)
+        nc.vector.reciprocal(out=root_inv[:], in_=root0[:])
+        interleave_filters(1)
+        nc.vector.scalar_tensor_tensor(
+            out=half_quot[:], in0=w_abs[:], scalar=0.5, in1=root_inv[:], op0=ALU.mult, op1=ALU.mult
+        )
+        turn_x(0, 1)
+        turn_x(1, 0, "l_bank")
+        copy_x(0, 0, True)
+        quantize(f_codes[:], f_scales[:], f_grouped[:])
+        quantize_x(0, 0, 2)
+        nc.vector.scalar_tensor_tensor(
+            out=root[:], in0=root0[:], scalar=0.5, in1=half_quot[:], op0=ALU.mult, op1=ALU.add
+        )
+        copy_x(0, 1, True)
+        filter_pass(0, 0)
+        filter_pass(0, 1)
+        copy_x(1, 0, False)
+        quantize_x(0, 2, 4)
+        filter_pass(0, 2)
+        filter_pass(0, 3)
+        quantize_x(1, 0, 2)
+        turn_x(1, 1)
+        square(0, 0)
+        filter_pass(1, 0)
+        square(0, 1)
+        filter_pass(1, 1)
+        copy_x(1, 1, False)
+        turn_x(2, 0)
+        turn_x(2, 1, "l_bank")
+        quantize_x(1, 2, 4)
+        square(0, 2)
+        filter_pass(1, 2)
+        square(0, 3)
+        filter_pass(1, 3)
+        copy_x(2, 0, False)
+        copy_x(2, 1, False)
+        turn_x(3, 0)
+        turn_x(3, 1)
+        quantize_x(2)
+        square(1, 0)
+        filter_pass(2, 0)
+        square(1, 1)
+        filter_pass(2, 1)
+        turn_averaging()
+        interleave_p(0)
+        square(1, 2)
+        filter_pass(2, 2)
+        square(1, 3)
+        filter_pass(2, 3)
+        copy_x(3, 0, True)
+        copy_x(3, 1, False)
+        quantize_p(0)
+        turn_x(4, 0)
+        turn_x(4, 1)
+        quantize_x(3)
+        square(2, 0)
+        filter_pass(3, 0)
+        square(2, 1)
+        filter_pass(3, 1)
+        copy_averaging()
+        interleave_p(1)
+        copy_x(4, 0, True)
+        copy_x(4, 1, False)
+        turn_x(5, 0)
+        turn_x(5, 1)
+        sign_averaging()
+        quantize_p(1)
+        square(2, 2)
+        filter_pass(3, 2)
+        square(2, 3)
+        filter_pass(3, 3)
+        quantize_x(4)
+        quantize(a_codes[:], a_scales[:], a_signed[:])
+        copy_x(5, 0, True)
+        copy_x(5, 1, False)
+
+        last = UNITS - 1
+        for u in range(3, last):
             odd = u % 2 == 1
-            early = (u - 2) // 2 if not odd else -1
-            middle = (u - 3) // 2 if odd else -1
-            late = (u - 4) // 2 if not odd else -1
-            quantize_x(u + 1, 0)
+            i = (u - 3) // 2 if odd else -1
+            k = (u - 4) // 2 if not odd else -1
             square(u, 0)
             filter_pass(u + 1, 0)
-            if u == 0:
-                sign_averaging()
+            turn_x(u + 3, 0)
+            turn_x(u + 3, 1)
             interleave_p(u - 1)
-            turn_x(u + 2, 0)
-            take_log(middle, (0, 1))
+            take_log(k, (0, 1, 2, 3))
+            store_y(i - 2)
             square(u, 1)
             filter_pass(u + 1, 1)
-            turn_x(u + 2, 1)
-            quantize_x(u + 1, 1)
-            round_y(late)
-            take_log(middle, (2, 3))
-            store_y(late)
-            if u == 0:
-                quantize(a_codes[:], a_scales[:], a_signed[:])
+            quantize_x(u + 2)
             quantize_p(u - 1)
             square(u, 2)
             filter_pass(u + 1, 2)
-            average(early)
-            gain_and_bias(middle)
-            quantize_y(late)
-            copy_x(u + 2, 0, True)
+            average(i)
+            turn_y(k - 1)
+            gain_and_bias(i - 1)
+            quantize_y(i - 2)
+            round_y(k - 1)
+            copy_x(u + 3, 0, True)
+            if u in (3,):
+                copy_x(u + 3, 1, True)
             square(u, 3)
             filter_pass(u + 1, 3)
-            turn_y(middle)
-            copy_x(u + 2, 1, False)
+            if u not in (3,):
+                copy_x(u + 3, 1, False)
+
+        i = B - 1
+        average(i - 1)
+        interleave_p(last - 1)
+        for j in range(PACK):
+            square(last, j, 0, 2)
+        gain_and_bias(i - 2)
+        quantize_p(last - 1)
+        for j in range(PACK):
+            square(last, j, 2, 4)
+        interleave_p(last, 0, 2)
+        store_y(i - 3)
+        turn_y(i - 2)
+        quantize_y(i - 3)
+        take_log(i - 1, (0, 1, 2, 3))
+        quantize_p(last, 0, 2)
+        average(i, 0, 2, "x_bank_1")
+        interleave_p(last, 2, 4)
+        store_y(i - 2)
+        gain_and_bias(i - 1)
+        turn_y(i - 1)
+        quantize_p(last, 2, 4)
+        average(i, 2, 4, "x_bank_0")
+        take_log(i, (0, 1))
+        round_y(i - 2)
+        store_y(i - 1)
+        gain_and_bias(i, 0, 2)
+        turn_y(i, 0, 2, "s_bank_0")
+        take_log(i, (2, 3))
+        round_y(i - 1)
+        quantize_y(i - 2)
+        gain_and_bias(i, 2, 4)
+        turn_y(i, 2, 4)
+        quantize_y(i - 1)
+        round_y(i)
+        store_y(i)
+        quantize_y(i)

@@ -25,8 +25,8 @@ SQRT_FLOOR = 2.0 ** -116
 
 def interleave_views(dst, src):
     return (
-        dst.rearrange("p (c i t) -> p c t i", i=4, t=PACK),
-        src.rearrange("p t (c i) -> p c t i", i=4),
+        dst.rearrange("p (g c i t) -> p g c t i", g=src.shape[1], i=4, t=PACK),
+        src.rearrange("p g t (c i) -> p g c t i", i=4),
     )
 
 
@@ -78,8 +78,27 @@ def tile_motor_imagery_log_power_h3_kernel(
 
         ident = keep.tile([P, P], F32)
         make_identity(nc, ident[:])
+        warm_in = keep.tile([P, 2 * SPAN], BF16, align_bytes=64)
+        warm_codes = keep.tile([P, 2 * P], U32, align_bytes=64)
+        warm_scales = keep.tile([P, 2 * P], U8, align_bytes=64)
+
+        def warm_up(passes, tag="s_bank_3"):
+            warm_bank = psum.tile([P, 2 * P], F32, name="warm_bank", tag=tag)
+            for k in range(passes):
+                nc.tensor.matmul_mx(
+                    out=warm_bank[:],
+                    lhsT=warm_codes[:, 0:P].bitcast(FP8X4),
+                    lhsT_scale=warm_scales[:, 0:P],
+                    rhs=warm_codes[:].bitcast(FP8X4),
+                    rhs_scale=warm_scales[:],
+                    start=True,
+                    stop=True,
+                )
+
+        nc.vector.memset(warm_in[:], 1.0)
         one = keep.tile([P, 1], F32)
         nc.vector.memset(one[:], 1.0)
+        nc.vector.quantize_mx(out=warm_codes[:].bitcast(FP8X4), scales=warm_scales[:], in_=warm_in[:])
 
         w = w_raw[:, :, 0:PACK]
         w_abs = keep.tile([P, HALVES, PACK], F32)
@@ -87,15 +106,13 @@ def tile_motor_imagery_log_power_h3_kernel(
         root_inv = keep.tile([P, HALVES, PACK], F32)
         half_quot = keep.tile([P, HALVES, PACK], F32)
         root = keep.tile([P, HALVES, PACK], F32)
-        w_neg = keep.tile([P, HALVES, PACK], F32)
         w_ge = keep.tile([P, HALVES, PACK], F32)
         w_sign = keep.tile([P, HALVES, PACK], BF16)
         warm = keep.tile([P, 1], F32)
-        nc.vector.tensor_scalar(out=w_neg[:], in0=w, scalar1=-1.0, scalar2=SQRT_FLOOR, op0=ALU.mult, op1=ALU.max)
+        nc.vector.scalar_tensor_tensor(out=w_abs[:], in0=w, scalar=-1.0, in1=w, op0=ALU.mult, op1=ALU.max)
         nc.vector.tensor_scalar(out=w_ge[:], in0=w, scalar1=0.0, scalar2=2.0, op0=ALU.is_ge, op1=ALU.mult)
-        nc.vector.tensor_tensor(out=w_abs[:], in0=w_neg[:], in1=w, op=ALU.max)
+        nc.scalar.activation(out=root0[:], in_=w_abs[:], func=ACT.Sqrt, bias=SQRT_FLOOR)
         nc.vector.tensor_scalar(out=w_sign[:], in0=w_ge[:], scalar1=-1.0, scalar2=None, op0=ALU.add)
-        nc.scalar.activation(out=root0[:], in_=w_abs[:], func=ACT.Sqrt)
         nc.scalar.activation(out=warm[:], in_=one[:], func=ACT.Ln)
 
         def quantize(codes, scales, grouped):
@@ -125,9 +142,11 @@ def tile_motor_imagery_log_power_h3_kernel(
         def copy_x(u, h, on_scalar):
             if not 0 <= u < UNITS:
                 return
-            if u not in x_grouped:
-                x_grouped[u] = work.tile([P, PACK * SPAN], BF16, name="x_grouped", tag="x_grouped", align_bytes=64)
-            dst = x_grouped[u][:, 2 * SPAN * h : 2 * SPAN * (h + 1)].bitcast(F32)
+            i, g = divmod(u, HALVES)
+            if i not in x_grouped:
+                x_grouped[i] = work.tile([P, T * PACK], BF16, name="x_grouped", tag="x_grouped", bufs=4, align_bytes=64)
+            first = PACK * SPAN * g + 2 * SPAN * h
+            dst = x_grouped[i][:, first : first + 2 * SPAN].bitcast(F32)
             dst = dst.rearrange("p (j m e) -> p j m e", j=2, e=2)
             src = x_bank[u, h][:].rearrange("p j e m -> p j m e")
             if on_scalar:
@@ -135,24 +154,25 @@ def tile_motor_imagery_log_power_h3_kernel(
             else:
                 nc.vector.tensor_copy(out=dst, in_=src)
 
-        def quantize_x(u, j0=0, j1=PACK):
-            if not 0 <= u < UNITS:
+        def quantize_x(i, j0=0, j1=HALVES * PACK):
+            if not 0 <= i < B:
                 return
             if j0 == 0:
-                x_codes[u] = work.tile([P, SPAN], U32, name="x_codes", tag="x_codes", align_bytes=64)
-                x_scales[u] = work.tile([P, SPAN], U8, name="x_scales", tag="x_scales", align_bytes=64)
+                x_codes[i] = work.tile([P, T], U32, name="x_codes", tag="x_codes", align_bytes=64)
+                x_scales[i] = work.tile([P, T], U8, name="x_scales", tag="x_scales", align_bytes=64)
             cols = slice(P * j0, P * j1)
-            quantize(x_codes[u][:, cols], x_scales[u][:, cols], x_grouped[u][:, SPAN * j0 : SPAN * j1])
+            quantize(x_codes[i][:, cols], x_scales[i][:, cols], x_grouped[i][:, SPAN * j0 : SPAN * j1])
 
         def filter_pass(u, j):
             if not 0 <= u < UNITS:
                 return
+            i, g = divmod(u, HALVES)
             s_bank[u, j] = psum.tile([P, F], F32, name="s_bank", tag="s_bank_%d" % j)
-            cols = slice(P * j, P * (j + 1))
+            cols = slice(SPAN * g + P * j, SPAN * g + P * (j + 1))
             nc.tensor.matmul_mx(
                 out=s_bank[u, j][:],
-                lhsT=x_codes[u][:, cols].bitcast(FP8X4),
-                lhsT_scale=x_scales[u][:, cols],
+                lhsT=x_codes[i][:, cols].bitcast(FP8X4),
+                lhsT_scale=x_scales[i][:, cols],
                 rhs=f_codes[:].bitcast(FP8X4),
                 rhs_scale=f_scales[:],
                 start=True,
@@ -162,60 +182,74 @@ def tile_motor_imagery_log_power_h3_kernel(
         def square(u, j, s0=0, s1=PACK):
             if not 0 <= u < UNITS:
                 return
-            if u not in p_rows:
-                p_rows[u] = work.tile([P, PACK, F], BF16, name="p_rows", tag="p_rows")
+            i, g = divmod(u, HALVES)
+            if i not in p_rows:
+                p_rows[i] = work.tile([P, HALVES, PACK, F], BF16, name="p_rows", tag="p_rows", bufs=4)
             cols = slice(P * s0, P * s1)
             nc.scalar.activation(
-                out=p_rows[u][:, j, cols],
+                out=p_rows[i][:, g, j, cols],
                 in_=s_bank[u, j][:, cols],
                 func=ACT.Square,
-                scale=root[:, u % HALVES, j : j + 1],
+                scale=root[:, g, j : j + 1],
             )
 
-        def interleave_p(u, s0=0, s1=PACK):
-            if not 0 <= u < UNITS:
-                return
-            if s0 == 0:
-                p_grouped[u] = work.tile([P, PACK * F], BF16, name="p_grouped", tag="p_grouped", align_bytes=64)
-            dst, src = interleave_views(p_grouped[u][:, SPAN * s0 : SPAN * s1], p_rows[u][:, :, P * s0 : P * s1])
-            nc.vector.tensor_copy(out=dst, in_=src)
-
-        def quantize_p(u, s0=0, s1=PACK):
-            if not 0 <= u < UNITS:
-                return
-            if s0 == 0:
-                p_codes[u] = work.tile([P, F], U32, name="p_codes", tag="p_codes", bufs=4, align_bytes=64)
-                p_scales[u] = work.tile([P, F], U8, name="p_scales", tag="p_scales", bufs=4, align_bytes=64)
-            cols = slice(P * s0, P * s1)
-            quantize(p_codes[u][:, cols], p_scales[u][:, cols], p_grouped[u][:, SPAN * s0 : SPAN * s1])
-
-        def average(i, s0=0, s1=PACK, tag="l_bank"):
+        def interleave_p(i, c0=0, c1=HALVES * PACK, on_scalar=False):
             if not 0 <= i < B:
                 return
-            bank = psum.tile([P, PACK, R], F32, name="l_bank", tag=tag)
-            for s in range(s0, s1):
-                l_bank[i, s] = bank
-                cols = slice(P * s, P * (s + 1))
+            if c0 == 0:
+                p_grouped[i] = work.tile([P, HALVES * PACK * F], BF16, name="p_grouped", tag="p_grouped", bufs=2, align_bytes=64)
+            g0, g1 = c0 // PACK, (c1 - 1) // PACK + 1
+            s0, s1 = c0 - PACK * g0, c1 - PACK * (g1 - 1)
+            dst, src = interleave_views(p_grouped[i][:, SPAN * c0 : SPAN * c1], p_rows[i][:, g0:g1, :, P * s0 : P * s1])
+            if on_scalar:
+                nc.scalar.copy(out=dst, in_=src)
+            else:
+                nc.vector.tensor_copy(out=dst, in_=src)
+
+        def quantize_p(i, c0=0, c1=HALVES * PACK):
+            if not 0 <= i < B:
+                return
+            if c0 == 0:
+                p_codes[i] = work.tile([P, HALVES * F], U32, name="p_codes", tag="p_codes", align_bytes=64)
+                p_scales[i] = work.tile([P, HALVES * F], U8, name="p_scales", tag="p_scales", align_bytes=64)
+            cols = slice(P * c0, P * c1)
+            quantize(p_codes[i][:, cols], p_scales[i][:, cols], p_grouped[i][:, SPAN * c0 : SPAN * c1])
+
+        def average_pass(i, s, g):
+            cols = slice(F * g + P * s, F * g + P * (s + 1))
+            windows = slice(R * g, R * (g + 1))
+            nc.tensor.matmul_mx(
+                out=l_bank[i, s],
+                lhsT=p_codes[i][:, cols].bitcast(FP8X4),
+                lhsT_scale=p_scales[i][:, cols],
+                rhs=a_codes[:, windows].bitcast(FP8X4),
+                rhs_scale=a_scales[:, windows],
+                start=(g == 0),
+                stop=(g == HALVES - 1),
+            )
+
+        def average(i):
+            if not 0 <= i < B:
+                return
+            bank = psum.tile([P, PACK, R], F32, name="l_bank", tag="l_bank")
+            for s in range(PACK):
+                l_bank[i, s] = bank[:, s, :]
                 for g in range(HALVES):
-                    windows = slice(R * g, R * (g + 1))
-                    nc.tensor.matmul_mx(
-                        out=bank[:, s, :],
-                        lhsT=p_codes[HALVES * i + g][:, cols].bitcast(FP8X4),
-                        lhsT_scale=p_scales[HALVES * i + g][:, cols],
-                        rhs=a_codes[:, windows].bitcast(FP8X4),
-                        rhs_scale=a_scales[:, windows],
-                        start=(g == 0),
-                        stop=(g == HALVES - 1),
-                    )
+                    average_pass(i, s, g)
+
+        def open_average(i, s, tag):
+            bank = psum.tile([P, R], F32, name="l_open", tag=tag)
+            l_bank[i, s] = bank[:]
+            average_pass(i, s, 0)
 
         def take_log(i, slots):
             if not 0 <= i < B:
                 return
-            if slots[0] == 0:
-                log_power[i] = work.tile([P, PACK, R], F32, name="log_power", tag="log_power")
+            if i not in log_power:
+                log_power[i] = work.tile([P, PACK, R], F32, name="log_power", tag="log_power", bufs=4)
             for s in slots:
                 nc.scalar.activation(
-                    out=log_power[i][:, s, :], in_=l_bank[i, s][:, s, :], func=ACT.Ln, bias=offset_col[:, s : s + 1]
+                    out=log_power[i][:, s, :], in_=l_bank[i, s], func=ACT.Ln, bias=offset_col[:, s : s + 1]
                 )
 
         def gain_and_bias(i, s0=0, s1=PACK):
@@ -223,7 +257,7 @@ def tile_motor_imagery_log_power_h3_kernel(
                 return
             if s0 == 0:
                 y_rows[i] = work.tile([P, PACK, R], F32, name="y_rows", tag="y_rows")
-            for s in range(s0, s1):
+            for s in reversed(range(s0, s1)):
                 nc.vector.tensor_scalar(
                     out=y_rows[i][:, s, :],
                     in0=log_power[i][:, s, :],
@@ -237,7 +271,7 @@ def tile_motor_imagery_log_power_h3_kernel(
             if not 0 <= i < B:
                 return
             y_grouped[i] = work.tile([P, PACK * R], BF16, name="y_grouped", tag="y_grouped", align_bytes=64)
-            dst, src = interleave_views(y_grouped[i][:], y_rows[i][:])
+            dst, src = interleave_views(y_grouped[i][:], y_rows[i][:].unsqueeze(1))
             nc.vector.tensor_copy(out=dst, in_=src)
 
         def quantize_y(i):
@@ -245,15 +279,21 @@ def tile_motor_imagery_log_power_h3_kernel(
                 return
             cols = slice(R * i, R * (i + 1))
             quantize(y_codes[:, cols], y_scales[:, cols], y_grouped[i][:])
+
+        def store_codes(i0, i1):
+            if i0 < 0:
+                return
+            cols = slice(R * i0, R * i1)
             nc.sync.dma_start(
                 out=out_1[0].rearrange("p m t -> p (m t)").bitcast(I32)[:, cols], in_=y_codes[:, cols].bitcast(I32)
             )
-            if i == B - 1:
-                for q in range(4):
-                    nc.sync.dma_start(
-                        out=out_2[0, 4 * q : 4 * q + 4, :].bitcast(I32),
-                        in_=y_scales[32 * q : 32 * q + 4, :].bitcast(I32),
-                    )
+
+        def store_scales():
+            for q in range(4):
+                nc.sync.dma_start(
+                    out=out_2[0, 4 * q : 4 * q + 4, :].bitcast(I32),
+                    in_=y_scales[32 * q : 32 * q + 4, :].bitcast(I32),
+                )
 
         def turn_y(i, s0=0, s1=PACK, tag="y_bank"):
             if not 0 <= i < B:
@@ -263,17 +303,20 @@ def tile_motor_imagery_log_power_h3_kernel(
             for s in range(s0, s1):
                 nc.tensor.transpose(y_bank[i][:, s, :], y_rows[i][:, s, :], ident[:])
 
-        def store_y(i, on_scalar=True):
+        def store_y(i, on_scalar=True, pieces=1):
             if not 0 <= i < B:
                 return
-            y_out = work.tile([P, F], F32, name="y_out", tag="y_out")
-            dst = y_out[:].rearrange("r (p s) -> r p s", s=PACK)
-            src = y_bank[i][:].rearrange("r s p -> r p s")
-            if on_scalar:
-                nc.scalar.copy(out=dst, in_=src)
-            else:
-                nc.vector.tensor_copy(out=dst, in_=src)
-            nc.sync.dma_start(out=out_0[i], in_=y_out[:])
+            y_out = work.tile([P, F], F32, name="y_out", tag="y_out", bufs=B)
+            width = P // pieces
+            for n in range(pieces):
+                part = y_out[:, PACK * width * n : PACK * width * (n + 1)]
+                dst = part.rearrange("r (p s) -> r p s", s=PACK)
+                src = y_bank[i][:, :, width * n : width * (n + 1)].rearrange("r s p -> r p s")
+                if on_scalar:
+                    nc.scalar.copy(out=dst, in_=src)
+                else:
+                    nc.vector.tensor_copy(out=dst, in_=src)
+                nc.sync.dma_start(out=out_0[i, :, PACK * width * n : PACK * width * (n + 1)], in_=part)
 
         f_grouped = keep.tile([P, PACK * F], BF16, align_bytes=64)
         a_turned = keep.tile([P, T], BF16, align_bytes=64)
@@ -309,7 +352,9 @@ def tile_motor_imagery_log_power_h3_kernel(
                 op=ALU.mult,
             )
 
+        warm_up(7)
         turn_x(0, 0)
+        warm_up(4)
         interleave_filters(0)
         nc.vector.reciprocal(out=root_inv[:], in_=root0[:])
         interleave_filters(1)
@@ -327,130 +372,145 @@ def tile_motor_imagery_log_power_h3_kernel(
         copy_x(0, 1, True)
         filter_pass(0, 0)
         filter_pass(0, 1)
-        copy_x(1, 0, False)
+        turn_x(1, 1, "y_bank")
+        copy_x(1, 0, True)
         quantize_x(0, 2, 4)
+        copy_x(1, 1, False)
         filter_pass(0, 2)
         filter_pass(0, 3)
-        quantize_x(1, 0, 2)
-        turn_x(1, 1)
+        turn_x(2, 0)
+        turn_x(2, 1)
+        quantize_x(0, 4, 8)
         square(0, 0)
         filter_pass(1, 0)
         square(0, 1)
         filter_pass(1, 1)
-        copy_x(1, 1, False)
-        turn_x(2, 0)
-        turn_x(2, 1, "l_bank")
-        quantize_x(1, 2, 4)
+        copy_x(2, 0, False)
+        copy_x(2, 1, False)
         square(0, 2)
         filter_pass(1, 2)
         square(0, 3)
         filter_pass(1, 3)
-        copy_x(2, 0, False)
-        copy_x(2, 1, False)
         turn_x(3, 0)
         turn_x(3, 1)
-        quantize_x(2)
+        quantize_x(1, 0, 4)
         square(1, 0)
         filter_pass(2, 0)
         square(1, 1)
         filter_pass(2, 1)
         turn_averaging()
-        interleave_p(0)
+        interleave_p(0, 0, 4)
         square(1, 2)
         filter_pass(2, 2)
-        square(1, 3)
-        filter_pass(2, 3)
         copy_x(3, 0, True)
         copy_x(3, 1, False)
-        quantize_p(0)
         turn_x(4, 0)
+        square(1, 3)
+        filter_pass(2, 3)
         turn_x(4, 1)
-        quantize_x(3)
+        interleave_p(0, 4, 8)
+        quantize_x(1, 4, 8)
         square(2, 0)
         filter_pass(3, 0)
+        copy_averaging()
         square(2, 1)
         filter_pass(3, 1)
-        copy_averaging()
-        interleave_p(1)
+        copy_x(4, 1, True)
         copy_x(4, 0, True)
-        copy_x(4, 1, False)
         turn_x(5, 0)
-        turn_x(5, 1)
+        quantize_p(0)
         sign_averaging()
-        quantize_p(1)
         square(2, 2)
         filter_pass(3, 2)
+        turn_x(5, 1)
+        quantize_x(2, 0, 4)
         square(2, 3)
         filter_pass(3, 3)
-        quantize_x(4)
-        quantize(a_codes[:], a_scales[:], a_signed[:])
         copy_x(5, 0, True)
         copy_x(5, 1, False)
+        quantize(a_codes[:], a_scales[:], a_signed[:])
 
         last = UNITS - 1
         for u in range(3, last):
             odd = u % 2 == 1
-            i = (u - 3) // 2 if odd else -1
-            k = (u - 4) // 2 if not odd else -1
-            square(u, 0)
-            filter_pass(u + 1, 0)
+            order = (0, 1, 2, 3)
+            k = (u - 3) // 2 if odd else (u - 4) // 2
+            done, half = divmod(u - 1, HALVES)
+            ahead, part = divmod(u + 2, HALVES)
+            square(u, order[0])
+            filter_pass(u + 1, order[0])
             turn_x(u + 3, 0)
             turn_x(u + 3, 1)
-            interleave_p(u - 1)
-            take_log(k, (0, 1, 2, 3))
-            store_y(i - 2)
-            square(u, 1)
-            filter_pass(u + 1, 1)
-            quantize_x(u + 2)
-            quantize_p(u - 1)
-            square(u, 2)
-            filter_pass(u + 1, 2)
-            average(i)
-            turn_y(k - 1)
-            gain_and_bias(i - 1)
-            quantize_y(i - 2)
-            round_y(k - 1)
+            interleave_p(done, PACK * half, PACK * (half + 1))
+            if odd:
+                store_y(k - 2, True)
+            else:
+                take_log(k, (0, 1, 2, 3))
+            square(u, order[1])
+            filter_pass(u + 1, order[1])
+            if odd:
+                quantize_x(ahead, PACK * part, PACK * (part + 1))
+                gain_and_bias(k - 1)
+                quantize_y(k - 2)
+                store_codes(k - 2, k - 1)
+            else:
+                round_y(k - 1)
+                quantize_p(done)
+                quantize_x(ahead, PACK * part, PACK * (part + 1))
+            square(u, order[2])
+            filter_pass(u + 1, order[2])
+            if odd:
+                average(k)
+            else:
+                turn_y(k - 1)
             copy_x(u + 3, 0, True)
-            if u in (3,):
+            if u in ():
                 copy_x(u + 3, 1, True)
-            square(u, 3)
-            filter_pass(u + 1, 3)
-            if u not in (3,):
+            square(u, order[3])
+            filter_pass(u + 1, order[3])
+            if u not in ():
                 copy_x(u + 3, 1, False)
 
         i = B - 1
         average(i - 1)
-        interleave_p(last - 1)
+        interleave_p(i, 0, 4)
         for j in range(PACK):
             square(last, j, 0, 2)
         gain_and_bias(i - 2)
-        quantize_p(last - 1)
+        turn_y(i - 2, 0, 4, "x_bank_0")
+        quantize_p(i, 0, 4)
         for j in range(PACK):
             square(last, j, 2, 4)
-        interleave_p(last, 0, 2)
-        store_y(i - 3)
-        turn_y(i - 2)
-        quantize_y(i - 3)
+        for s in range(PACK):
+            open_average(i, s, "s_bank_%d" % s)
+        interleave_p(i, 4, 6)
         take_log(i - 1, (0, 1, 2, 3))
-        quantize_p(last, 0, 2)
-        average(i, 0, 2, "x_bank_1")
-        interleave_p(last, 2, 4)
+        interleave_p(i, 6, 8)
+        quantize_p(i, 4, 6)
+        average_pass(i, 0, 1)
+        average_pass(i, 1, 1)
+        quantize_p(i, 6, 8)
+        average_pass(i, 2, 1)
+        average_pass(i, 3, 1)
+        store_y(i - 3)
         store_y(i - 2)
         gain_and_bias(i - 1)
-        turn_y(i - 1)
-        quantize_p(last, 2, 4)
-        average(i, 2, 4, "x_bank_0")
-        take_log(i, (0, 1))
+        turn_y(i - 1, 0, 4, "x_bank_1")
+        take_log(i, (1, 0))
+        take_log(i, (3, 2))
+        quantize_y(i - 3)
+        store_codes(i - 3, i - 2)
         round_y(i - 2)
-        store_y(i - 1)
         gain_and_bias(i, 0, 2)
-        turn_y(i, 0, 2, "s_bank_0")
-        take_log(i, (2, 3))
-        round_y(i - 1)
-        quantize_y(i - 2)
+        turn_y(i, 0, 2, "l_bank")
         gain_and_bias(i, 2, 4)
         turn_y(i, 2, 4)
-        quantize_y(i - 1)
+        store_y(i - 1, True)
+        round_y(i - 1)
+        quantize_y(i - 2)
         round_y(i)
+        quantize_y(i - 1)
         store_y(i)
         quantize_y(i)
+        store_codes(i - 2, B)
+        store_scales()

@@ -20,13 +20,21 @@ PACK = 4
 SPAN = P * PACK
 HALVES = T // SPAN
 UNITS = B * HALVES
+PAIR = 2
+WORDS = SPAN // 2
+RUN = 4
+PADDED = 16
 SQRT_FLOOR = 2.0 ** -116
+LOOKAHEAD = 3
+RAMP = 3
+WARM_FIRST, WARM_SECOND = 7, 4
+SLACK_BUFS = 4
 
 
 def interleave_views(dst, src):
     return (
-        dst.rearrange("p (g c i t) -> p g c t i", g=src.shape[1], i=4, t=PACK),
-        src.rearrange("p g t (c i) -> p g c t i", i=4),
+        dst.rearrange("p (c i j) -> p c j i", i=RUN, j=PACK),
+        src.rearrange("p j (c i) -> p c j i", i=RUN),
     )
 
 
@@ -41,221 +49,212 @@ def tile_motor_imagery_log_power_h3_kernel(
         ctx.enter_context(tc.manual_schedule())
 
         x_rows = x.rearrange("b (g p j) c -> (b g) p j c", g=HALVES, j=PACK)
-        x_raw = {}
+        x_raw, f_raw = {}, {}
 
         def load_x(u, h):
-            x_raw[u, h] = keep.tile([P, 2 * C], BF16, name="x_raw_%d_%d" % (u, h))
+            x_raw[u, h] = keep.tile([P, PAIR * C], BF16, name="x_raw_%d_%d" % (u, h))
             nc.sync.dma_start(
-                out=x_raw[u, h][:].rearrange("p (j c) -> p j c", j=2), in_=x_rows[u, :, 2 * h : 2 * h + 2, :]
+                out=x_raw[u, h][:].rearrange("p (j c) -> p j c", j=PAIR),
+                in_=x_rows[u, :, PAIR * h : PAIR * (h + 1), :],
             )
 
-        w_raw = keep.tile([P, HALVES, 16], BF16)
-        nc.sync.dma_start(out=w_raw[:, :, 0:PACK], in_=sample_weights.rearrange("(g p j) -> p g j", g=HALVES, j=PACK))
-        load_x(0, 0)
-        f_raw = {}
+        w_raw = keep.tile([P, HALVES, PADDED], BF16)
+        w = w_raw[:, :, 0:PACK]
+        nc.sync.dma_start(out=w, in_=sample_weights.rearrange("(g p j) -> p g j", g=HALVES, j=PACK))
         for h in range(2):
             f_raw[h] = keep.tile([P, PACK, F // 2], BF16, name="f_raw_%d" % h)
             nc.sync.dma_start(
                 out=f_raw[h][:], in_=filters.rearrange("(p j) f -> p j f", j=PACK)[:, :, h * F // 2 : (h + 1) * F // 2]
             )
-        load_x(0, 1)
-        load_x(1, 0)
-        load_x(1, 1)
-        load_x(2, 0)
-        load_x(2, 1)
+            load_x(0, h)
+        for u in range(1, RAMP):
+            load_x(u, 0)
+            load_x(u, 1)
         a_raw = keep.tile([P, T], BF16)
         nc.sync.dma_start(out=a_raw[:], in_=averaging)
-        load_x(3, 0)
-        load_x(3, 1)
+        load_x(RAMP, 0)
+        load_x(RAMP, 1)
         offset_col = keep.tile([P, PACK], BF16)
         gain_col = keep.tile([P, PACK], BF16)
         bias_col = keep.tile([P, PACK], BF16)
         for col, vec in ((offset_col, power_offset), (gain_col, gain), (bias_col, bias)):
             nc.sync.dma_start(out=col[:], in_=vec.rearrange("(p s) -> p s", s=PACK))
-        for u in range(4, UNITS):
+        for u in range(RAMP + 1, UNITS):
             load_x(u, 0)
             load_x(u, 1)
 
         ident = keep.tile([P, P], F32)
         make_identity(nc, ident[:])
-        warm_in = keep.tile([P, 2 * SPAN], BF16, align_bytes=64)
-        warm_codes = keep.tile([P, 2 * P], U32, align_bytes=64)
-        warm_scales = keep.tile([P, 2 * P], U8, align_bytes=64)
-
-        def warm_up(passes, tag="s_bank_3"):
-            warm_bank = psum.tile([P, 2 * P], F32, name="warm_bank", tag=tag)
-            for k in range(passes):
-                nc.tensor.matmul_mx(
-                    out=warm_bank[:],
-                    lhsT=warm_codes[:, 0:P].bitcast(FP8X4),
-                    lhsT_scale=warm_scales[:, 0:P],
-                    rhs=warm_codes[:].bitcast(FP8X4),
-                    rhs_scale=warm_scales[:],
-                    start=True,
-                    stop=True,
-                )
-
-        nc.vector.memset(warm_in[:], 1.0)
-        one = keep.tile([P, 1], F32)
-        nc.vector.memset(one[:], 1.0)
-        nc.vector.quantize_mx(out=warm_codes[:].bitcast(FP8X4), scales=warm_scales[:], in_=warm_in[:])
-
-        w = w_raw[:, :, 0:PACK]
-        w_abs = keep.tile([P, HALVES, PACK], F32)
-        root0 = keep.tile([P, HALVES, PACK], F32)
-        root_inv = keep.tile([P, HALVES, PACK], F32)
-        half_quot = keep.tile([P, HALVES, PACK], F32)
-        root = keep.tile([P, HALVES, PACK], F32)
-        w_ge = keep.tile([P, HALVES, PACK], F32)
-        w_sign = keep.tile([P, HALVES, PACK], BF16)
-        warm = keep.tile([P, 1], F32)
-        nc.vector.scalar_tensor_tensor(out=w_abs[:], in0=w, scalar=-1.0, in1=w, op0=ALU.mult, op1=ALU.max)
-        nc.vector.tensor_scalar(out=w_ge[:], in0=w, scalar1=0.0, scalar2=2.0, op0=ALU.is_ge, op1=ALU.mult)
-        nc.scalar.activation(out=root0[:], in_=w_abs[:], func=ACT.Sqrt, bias=SQRT_FLOOR)
-        nc.vector.tensor_scalar(out=w_sign[:], in0=w_ge[:], scalar1=-1.0, scalar2=None, op0=ALU.add)
-        nc.scalar.activation(out=warm[:], in_=one[:], func=ACT.Ln)
 
         def quantize(codes, scales, grouped):
             nc.vector.quantize_mx(out=codes.bitcast(FP8X4), scales=scales, in_=grouped)
 
-        x_bank, x_grouped, x_codes, x_scales = {}, {}, {}, {}
-        s_bank, p_rows, p_grouped, p_codes, p_scales = {}, {}, {}, {}, {}
-        l_bank, log_power, y_rows, y_grouped, y_bank = {}, {}, {}, {}, {}
+        def mx_pass(out, l_codes, l_scales, r_codes, r_scales, start=True, stop=True):
+            nc.tensor.matmul_mx(
+                out=out,
+                lhsT=l_codes.bitcast(FP8X4),
+                lhsT_scale=l_scales,
+                rhs=r_codes.bitcast(FP8X4),
+                rhs_scale=r_scales,
+                start=start,
+                stop=stop,
+            )
+
+        def copy(on_scalar, dst, src):
+            if on_scalar:
+                nc.scalar.copy(out=dst, in_=src)
+            else:
+                nc.vector.tensor_copy(out=dst, in_=src)
+
+        warm_in = keep.tile([P, PAIR * SPAN], BF16, align_bytes=64)
+        warm_codes = keep.tile([P, PAIR * P], U32, align_bytes=64)
+        warm_scales = keep.tile([P, PAIR * P], U8, align_bytes=64)
+        one = keep.tile([P, 1], F32)
+        nc.vector.memset(warm_in[:], 1.0)
+        nc.vector.memset(one[:], 1.0)
+        quantize(warm_codes[:], warm_scales[:], warm_in[:])
+
+        def warm_up(passes):
+            warm_bank = psum.tile([P, PAIR * P], F32, name="warm_bank", tag="s_bank_3")
+            for repeat in range(passes):
+                mx_pass(warm_bank[:], warm_codes[:, 0:P], warm_scales[:, 0:P], warm_codes[:], warm_scales[:])
+
+        w_abs = keep.tile([P, HALVES, PACK], F32)
+        guess = keep.tile([P, HALVES, PACK], F32)
+        guess_inv = keep.tile([P, HALVES, PACK], F32)
+        half_quot = keep.tile([P, HALVES, PACK], F32)
+        root = keep.tile([P, HALVES, PACK], F32)
+        w_ge = keep.tile([P, HALVES, PACK], F32)
+        w_sign = keep.tile([P, HALVES, PACK], BF16)
+        nc.vector.scalar_tensor_tensor(out=w_abs[:], in0=w, scalar=-1.0, in1=w, op0=ALU.mult, op1=ALU.max)
+        nc.vector.tensor_scalar(out=w_ge[:], in0=w, scalar1=0.0, scalar2=2.0, op0=ALU.is_ge, op1=ALU.mult)
+        nc.scalar.activation(out=guess[:], in_=w_abs[:], func=ACT.Sqrt, bias=SQRT_FLOOR)
+        nc.vector.tensor_scalar(out=w_sign[:], in0=w_ge[:], scalar1=-1.0, scalar2=None, op0=ALU.add)
+        table_warm = keep.tile([P, 1], F32)
+        nc.scalar.activation(out=table_warm[:], in_=one[:], func=ACT.Ln)
+
+        f_grouped = keep.tile([P, PACK * F], BF16, align_bytes=64)
         f_codes = keep.tile([P, F], U32, align_bytes=64)
         f_scales = keep.tile([P, F], U8, align_bytes=64)
+        a_turned = keep.tile([P, T], BF16, align_bytes=64)
+        a_signed = keep.tile([P, T], BF16, align_bytes=64)
         a_codes = keep.tile([P, HALVES * R], U32, align_bytes=64)
         a_scales = keep.tile([P, HALVES * R], U8, align_bytes=64)
         y_codes = keep.tile([P, B * R], U32, align_bytes=64)
         y_scales = keep.tile([P, B * R], U8, align_bytes=64)
+        x_bank, x_grouped, x_codes, x_scales = {}, {}, {}, {}
+        s_bank, p_rows, p_grouped, p_codes, p_scales = {}, {}, {}, {}, {}
+        l_sums, log_power, y_rows, y_grouped, y_bank = {}, {}, {}, {}, {}
 
-        def turn_x(u, h, tag=None):
-            if not 0 <= u < UNITS:
-                return
-            x_bank[u, h] = psum.tile([P, 2, 2, P], F32, name="x_bank", tag=tag or "x_bank_%d" % h)
-            words = x_raw[u, h][:].bitcast(F32)
-            for j in range(2):
+        def turn_words(bank, words):
+            for part in range(2):
                 for e in range(2):
                     nc.tensor.transpose(
-                        x_bank[u, h][:, j, e, :], words[:, 256 * j + e : 256 * (j + 1) : 2], ident[:]
+                        bank[:, part, e, :], words[:, WORDS * part + e : WORDS * (part + 1) : 2], ident[:]
                     )
 
-        def copy_x(u, h, on_scalar):
-            if not 0 <= u < UNITS:
-                return
-            i, g = divmod(u, HALVES)
-            if i not in x_grouped:
-                x_grouped[i] = work.tile([P, T * PACK], BF16, name="x_grouped", tag="x_grouped", bufs=4, align_bytes=64)
-            first = PACK * SPAN * g + 2 * SPAN * h
-            dst = x_grouped[i][:, first : first + 2 * SPAN].bitcast(F32)
-            dst = dst.rearrange("p (j m e) -> p j m e", j=2, e=2)
-            src = x_bank[u, h][:].rearrange("p j e m -> p j m e")
-            if on_scalar:
-                nc.scalar.copy(out=dst, in_=src)
-            else:
-                nc.vector.tensor_copy(out=dst, in_=src)
+        def join_words(on_scalar, grouped, bank):
+            dst = grouped.bitcast(F32).rearrange("p (part m e) -> p part m e", part=2, e=2)
+            copy(on_scalar, dst, bank.rearrange("p part e m -> p part m e"))
 
-        def quantize_x(i, j0=0, j1=HALVES * PACK):
-            if not 0 <= i < B:
-                return
-            if j0 == 0:
-                x_codes[i] = work.tile([P, T], U32, name="x_codes", tag="x_codes", align_bytes=64)
-                x_scales[i] = work.tile([P, T], U8, name="x_scales", tag="x_scales", align_bytes=64)
-            cols = slice(P * j0, P * j1)
-            quantize(x_codes[i][:, cols], x_scales[i][:, cols], x_grouped[i][:, SPAN * j0 : SPAN * j1])
+        def interleave_filters(h):
+            span = slice(h * P // 2, (h + 1) * P // 2)
+            nc.vector.tensor_copy(
+                out=f_grouped[:].rearrange("p (s m j) -> p m s j", s=PACK, j=PACK)[:, span],
+                in_=f_raw[h][:].rearrange("p j (m s) -> p m s j", s=PACK),
+            )
+
+        def turn_x(u, h, tag=None):
+            if u < UNITS:
+                x_bank[u, h] = psum.tile([P, PAIR, 2, P], F32, name="x_bank", tag=tag or "x_bank_%d" % h)
+                turn_words(x_bank[u, h], x_raw[u, h][:].bitcast(F32))
+
+        def copy_x(u, h, on_scalar):
+            if u < UNITS:
+                i, g = divmod(u, HALVES)
+                if i not in x_grouped:
+                    x_grouped[i] = work.tile(
+                        [P, T * PACK], BF16, name="x_grouped", tag="x_grouped", bufs=SLACK_BUFS, align_bytes=64
+                    )
+                first = SPAN * (PACK * g + PAIR * h)
+                join_words(on_scalar, x_grouped[i][:, first : first + PAIR * SPAN], x_bank[u, h][:])
+
+        def quantize_x(u, j0=0, j1=PACK):
+            if u < UNITS:
+                i, g = divmod(u, HALVES)
+                if i not in x_codes:
+                    x_codes[i] = work.tile([P, T], U32, name="x_codes", tag="x_codes", align_bytes=64)
+                    x_scales[i] = work.tile([P, T], U8, name="x_scales", tag="x_scales", align_bytes=64)
+                n0, n1 = PACK * g + j0, PACK * g + j1
+                cols = slice(P * n0, P * n1)
+                quantize(x_codes[i][:, cols], x_scales[i][:, cols], x_grouped[i][:, SPAN * n0 : SPAN * n1])
 
         def filter_pass(u, j):
-            if not 0 <= u < UNITS:
-                return
             i, g = divmod(u, HALVES)
             s_bank[u, j] = psum.tile([P, F], F32, name="s_bank", tag="s_bank_%d" % j)
             cols = slice(SPAN * g + P * j, SPAN * g + P * (j + 1))
-            nc.tensor.matmul_mx(
-                out=s_bank[u, j][:],
-                lhsT=x_codes[i][:, cols].bitcast(FP8X4),
-                lhsT_scale=x_scales[i][:, cols],
-                rhs=f_codes[:].bitcast(FP8X4),
-                rhs_scale=f_scales[:],
-                start=True,
-                stop=True,
-            )
+            mx_pass(s_bank[u, j][:], x_codes[i][:, cols], x_scales[i][:, cols], f_codes[:], f_scales[:])
 
         def square(u, j, s0=0, s1=PACK):
-            if not 0 <= u < UNITS:
-                return
             i, g = divmod(u, HALVES)
             if i not in p_rows:
-                p_rows[i] = work.tile([P, HALVES, PACK, F], BF16, name="p_rows", tag="p_rows", bufs=4)
+                p_rows[i] = work.tile([P, HALVES, PACK, F], BF16, name="p_rows", tag="p_rows", bufs=SLACK_BUFS)
             cols = slice(P * s0, P * s1)
             nc.scalar.activation(
-                out=p_rows[i][:, g, j, cols],
-                in_=s_bank[u, j][:, cols],
-                func=ACT.Square,
-                scale=root[:, g, j : j + 1],
+                out=p_rows[i][:, g, j, cols], in_=s_bank[u, j][:, cols], func=ACT.Square, scale=root[:, g, j : j + 1]
             )
 
-        def interleave_p(i, c0=0, c1=HALVES * PACK, on_scalar=False):
-            if not 0 <= i < B:
-                return
-            if c0 == 0:
-                p_grouped[i] = work.tile([P, HALVES * PACK * F], BF16, name="p_grouped", tag="p_grouped", bufs=2, align_bytes=64)
-            g0, g1 = c0 // PACK, (c1 - 1) // PACK + 1
-            s0, s1 = c0 - PACK * g0, c1 - PACK * (g1 - 1)
-            dst, src = interleave_views(p_grouped[i][:, SPAN * c0 : SPAN * c1], p_rows[i][:, g0:g1, :, P * s0 : P * s1])
-            if on_scalar:
-                nc.scalar.copy(out=dst, in_=src)
-            else:
-                nc.vector.tensor_copy(out=dst, in_=src)
+        def square_and_refill(u, j):
+            square(u, j)
+            filter_pass(u + 1, j)
 
-        def quantize_p(i, c0=0, c1=HALVES * PACK):
-            if not 0 <= i < B:
-                return
-            if c0 == 0:
+        def interleave_p(u, s0=0, s1=PACK):
+            i, g = divmod(u, HALVES)
+            if i not in p_grouped:
+                p_grouped[i] = work.tile(
+                    [P, HALVES * PACK * F], BF16, name="p_grouped", tag="p_grouped", bufs=2, align_bytes=64
+                )
+            dst = p_grouped[i][:, SPAN * (PACK * g + s0) : SPAN * (PACK * g + s1)]
+            dst, src = interleave_views(dst, p_rows[i][:, g, :, P * s0 : P * s1])
+            nc.vector.tensor_copy(out=dst, in_=src)
+
+        def quantize_p(i, n0=0, n1=HALVES * PACK):
+            if i not in p_codes:
                 p_codes[i] = work.tile([P, HALVES * F], U32, name="p_codes", tag="p_codes", align_bytes=64)
                 p_scales[i] = work.tile([P, HALVES * F], U8, name="p_scales", tag="p_scales", align_bytes=64)
-            cols = slice(P * c0, P * c1)
-            quantize(p_codes[i][:, cols], p_scales[i][:, cols], p_grouped[i][:, SPAN * c0 : SPAN * c1])
+            cols = slice(P * n0, P * n1)
+            quantize(p_codes[i][:, cols], p_scales[i][:, cols], p_grouped[i][:, SPAN * n0 : SPAN * n1])
 
         def average_pass(i, s, g):
             cols = slice(F * g + P * s, F * g + P * (s + 1))
             windows = slice(R * g, R * (g + 1))
-            nc.tensor.matmul_mx(
-                out=l_bank[i, s],
-                lhsT=p_codes[i][:, cols].bitcast(FP8X4),
-                lhsT_scale=p_scales[i][:, cols],
-                rhs=a_codes[:, windows].bitcast(FP8X4),
-                rhs_scale=a_scales[:, windows],
+            mx_pass(
+                l_sums[i, s],
+                p_codes[i][:, cols],
+                p_scales[i][:, cols],
+                a_codes[:, windows],
+                a_scales[:, windows],
                 start=(g == 0),
                 stop=(g == HALVES - 1),
             )
 
         def average(i):
-            if not 0 <= i < B:
-                return
-            bank = psum.tile([P, PACK, R], F32, name="l_bank", tag="l_bank")
+            l_bank = psum.tile([P, PACK, R], F32, name="l_bank", tag="l_bank")
             for s in range(PACK):
-                l_bank[i, s] = bank[:, s, :]
+                l_sums[i, s] = l_bank[:, s, :]
                 for g in range(HALVES):
                     average_pass(i, s, g)
 
-        def open_average(i, s, tag):
-            bank = psum.tile([P, R], F32, name="l_open", tag=tag)
-            l_bank[i, s] = bank[:]
-            average_pass(i, s, 0)
-
-        def take_log(i, slots):
-            if not 0 <= i < B:
-                return
+        def take_log(i, slots=range(PACK)):
             if i not in log_power:
-                log_power[i] = work.tile([P, PACK, R], F32, name="log_power", tag="log_power", bufs=4)
+                log_power[i] = work.tile([P, PACK, R], F32, name="log_power", tag="log_power", bufs=SLACK_BUFS)
             for s in slots:
                 nc.scalar.activation(
-                    out=log_power[i][:, s, :], in_=l_bank[i, s], func=ACT.Ln, bias=offset_col[:, s : s + 1]
+                    out=log_power[i][:, s, :], in_=l_sums[i, s], func=ACT.Ln, bias=offset_col[:, s : s + 1]
                 )
 
         def gain_and_bias(i, s0=0, s1=PACK):
-            if not 0 <= i < B:
-                return
-            if s0 == 0:
+            if i not in y_rows:
                 y_rows[i] = work.tile([P, PACK, R], F32, name="y_rows", tag="y_rows")
             for s in reversed(range(s0, s1)):
                 nc.vector.tensor_scalar(
@@ -268,244 +267,184 @@ def tile_motor_imagery_log_power_h3_kernel(
                 )
 
         def round_y(i):
-            if not 0 <= i < B:
-                return
             y_grouped[i] = work.tile([P, PACK * R], BF16, name="y_grouped", tag="y_grouped", align_bytes=64)
-            dst, src = interleave_views(y_grouped[i][:], y_rows[i][:].unsqueeze(1))
+            dst, src = interleave_views(y_grouped[i][:], y_rows[i][:])
             nc.vector.tensor_copy(out=dst, in_=src)
 
         def quantize_y(i):
-            if not 0 <= i < B:
-                return
             cols = slice(R * i, R * (i + 1))
             quantize(y_codes[:, cols], y_scales[:, cols], y_grouped[i][:])
 
         def store_codes(i0, i1):
-            if i0 < 0:
-                return
             cols = slice(R * i0, R * i1)
             nc.sync.dma_start(
-                out=out_1[0].rearrange("p m t -> p (m t)").bitcast(I32)[:, cols], in_=y_codes[:, cols].bitcast(I32)
+                out=out_1[0].rearrange("p m j -> p (m j)").bitcast(I32)[:, cols], in_=y_codes[:, cols].bitcast(I32)
             )
 
         def store_scales():
-            for q in range(4):
-                nc.sync.dma_start(
-                    out=out_2[0, 4 * q : 4 * q + 4, :].bitcast(I32),
-                    in_=y_scales[32 * q : 32 * q + 4, :].bitcast(I32),
+            for quadrant in range(4):
+                queue = nc.sync if quadrant < 2 else nc.scalar
+                queue.dma_start(
+                    out=out_2[0, 4 * quadrant : 4 * quadrant + 4, :].bitcast(I32),
+                    in_=y_scales[32 * quadrant : 32 * quadrant + 4, :].bitcast(I32),
                 )
 
         def turn_y(i, s0=0, s1=PACK, tag="y_bank"):
-            if not 0 <= i < B:
-                return
-            if s0 == 0:
+            if i not in y_bank:
                 y_bank[i] = psum.tile([P, PACK, P], F32, name="y_bank", tag=tag)
             for s in range(s0, s1):
                 nc.tensor.transpose(y_bank[i][:, s, :], y_rows[i][:, s, :], ident[:])
 
-        def store_y(i, on_scalar=True, pieces=1):
-            if not 0 <= i < B:
-                return
+        def store_y(i):
             y_out = work.tile([P, F], F32, name="y_out", tag="y_out", bufs=B)
-            width = P // pieces
-            for n in range(pieces):
-                part = y_out[:, PACK * width * n : PACK * width * (n + 1)]
-                dst = part.rearrange("r (p s) -> r p s", s=PACK)
-                src = y_bank[i][:, :, width * n : width * (n + 1)].rearrange("r s p -> r p s")
-                if on_scalar:
-                    nc.scalar.copy(out=dst, in_=src)
-                else:
-                    nc.vector.tensor_copy(out=dst, in_=src)
-                nc.sync.dma_start(out=out_0[i, :, PACK * width * n : PACK * width * (n + 1)], in_=part)
-
-        f_grouped = keep.tile([P, PACK * F], BF16, align_bytes=64)
-        a_turned = keep.tile([P, T], BF16, align_bytes=64)
-        a_signed = keep.tile([P, T], BF16, align_bytes=64)
-
-        def interleave_filters(h):
-            nc.vector.tensor_copy(
-                out=f_grouped[:].rearrange("p (s m j) -> p m s j", s=PACK, j=PACK)[:, 64 * h : 64 * (h + 1)],
-                in_=f_raw[h][:].rearrange("p j (m s) -> p m s j", s=PACK),
-            )
-
-        a_banks = []
-
-        def turn_averaging():
-            a_bank = psum.tile([P, HALVES, 2, R], F32, name="a_bank", tag="y_bank")
-            a_banks.append(a_bank)
-            a_words = a_raw[:].bitcast(F32)
-            for g in range(HALVES):
-                for e in range(2):
-                    nc.tensor.transpose(a_bank[:, g, e, :], a_words[:, 256 * g + e : 256 * (g + 1) : 2], ident[:])
-
-        def copy_averaging():
             nc.scalar.copy(
-                out=a_turned[:].bitcast(F32).rearrange("p (g r e) -> p g r e", g=HALVES, e=2),
-                in_=a_banks[0][:].rearrange("p g e r -> p g r e"),
+                out=y_out[:].rearrange("r (m s) -> r m s", s=PACK), in_=y_bank[i][:].rearrange("r s m -> r m s")
             )
+            nc.sync.dma_start(out=out_0[i], in_=y_out[:])
 
-        def sign_averaging():
-            nc.vector.tensor_tensor(
-                out=a_signed[:].rearrange("p (g r j) -> p g r j", g=HALVES, j=PACK),
-                in0=a_turned[:].rearrange("p (g r j) -> p g r j", g=HALVES, j=PACK),
-                in1=w_sign[:].unsqueeze(2).to_broadcast([P, HALVES, R, PACK]),
-                op=ALU.mult,
-            )
-
-        warm_up(7)
+        warm_up(WARM_FIRST)
         turn_x(0, 0)
-        warm_up(4)
+        warm_up(WARM_SECOND)
         interleave_filters(0)
-        nc.vector.reciprocal(out=root_inv[:], in_=root0[:])
+        nc.vector.reciprocal(out=guess_inv[:], in_=guess[:])
         interleave_filters(1)
         nc.vector.scalar_tensor_tensor(
-            out=half_quot[:], in0=w_abs[:], scalar=0.5, in1=root_inv[:], op0=ALU.mult, op1=ALU.mult
+            out=half_quot[:], in0=w_abs[:], scalar=0.5, in1=guess_inv[:], op0=ALU.mult, op1=ALU.mult
         )
         turn_x(0, 1)
         turn_x(1, 0, "l_bank")
         copy_x(0, 0, True)
         quantize(f_codes[:], f_scales[:], f_grouped[:])
-        quantize_x(0, 0, 2)
+        quantize_x(0, 0, PAIR)
         nc.vector.scalar_tensor_tensor(
-            out=root[:], in0=root0[:], scalar=0.5, in1=half_quot[:], op0=ALU.mult, op1=ALU.add
+            out=root[:], in0=guess[:], scalar=0.5, in1=half_quot[:], op0=ALU.mult, op1=ALU.add
         )
         copy_x(0, 1, True)
         filter_pass(0, 0)
         filter_pass(0, 1)
         turn_x(1, 1, "y_bank")
-        copy_x(1, 0, True)
-        quantize_x(0, 2, 4)
+        copy_x(1, 0, False)
+        quantize_x(0, PAIR, PACK)
         copy_x(1, 1, False)
         filter_pass(0, 2)
         filter_pass(0, 3)
+
         turn_x(2, 0)
         turn_x(2, 1)
-        quantize_x(0, 4, 8)
-        square(0, 0)
-        filter_pass(1, 0)
-        square(0, 1)
-        filter_pass(1, 1)
+        quantize_x(1)
+        square_and_refill(0, 0)
+        square_and_refill(0, 1)
         copy_x(2, 0, False)
         copy_x(2, 1, False)
-        square(0, 2)
-        filter_pass(1, 2)
-        square(0, 3)
-        filter_pass(1, 3)
+        square_and_refill(0, 2)
+        square_and_refill(0, 3)
+
         turn_x(3, 0)
         turn_x(3, 1)
-        quantize_x(1, 0, 4)
-        square(1, 0)
-        filter_pass(2, 0)
-        square(1, 1)
-        filter_pass(2, 1)
-        turn_averaging()
-        interleave_p(0, 0, 4)
-        square(1, 2)
-        filter_pass(2, 2)
+        quantize_x(2)
+        square_and_refill(1, 0)
+        square_and_refill(1, 1)
+        a_bank = psum.tile([P, HALVES, 2, R], F32, name="a_bank", tag="y_bank")
+        turn_words(a_bank, a_raw[:].bitcast(F32))
+        interleave_p(0)
+        square_and_refill(1, 2)
         copy_x(3, 0, True)
         copy_x(3, 1, False)
         turn_x(4, 0)
-        square(1, 3)
-        filter_pass(2, 3)
+        square_and_refill(1, 3)
+
         turn_x(4, 1)
-        interleave_p(0, 4, 8)
-        quantize_x(1, 4, 8)
-        square(2, 0)
-        filter_pass(3, 0)
-        copy_averaging()
-        square(2, 1)
-        filter_pass(3, 1)
+        interleave_p(1)
+        quantize_x(3)
+        square_and_refill(2, 0)
+        join_words(True, a_turned[:], a_bank[:])
+        square_and_refill(2, 1)
         copy_x(4, 1, True)
         copy_x(4, 0, True)
         turn_x(5, 0)
         quantize_p(0)
-        sign_averaging()
-        square(2, 2)
-        filter_pass(3, 2)
+        nc.vector.tensor_tensor(
+            out=a_signed[:].rearrange("p (g r j) -> p g r j", g=HALVES, j=PACK),
+            in0=a_turned[:].rearrange("p (g r j) -> p g r j", g=HALVES, j=PACK),
+            in1=w_sign[:].unsqueeze(2).to_broadcast([P, HALVES, R, PACK]),
+            op=ALU.mult,
+        )
+        square_and_refill(2, 2)
         turn_x(5, 1)
-        quantize_x(2, 0, 4)
-        square(2, 3)
-        filter_pass(3, 3)
+        quantize_x(4)
+        square_and_refill(2, 3)
+        quantize(a_codes[:], a_scales[:], a_signed[:])
         copy_x(5, 0, True)
         copy_x(5, 1, False)
-        quantize(a_codes[:], a_scales[:], a_signed[:])
 
         last = UNITS - 1
-        for u in range(3, last):
+        for u in range(RAMP, last):
             odd = u % 2 == 1
-            order = (0, 1, 2, 3)
-            k = (u - 3) // 2 if odd else (u - 4) // 2
-            done, half = divmod(u - 1, HALVES)
-            ahead, part = divmod(u + 2, HALVES)
-            square(u, order[0])
-            filter_pass(u + 1, order[0])
-            turn_x(u + 3, 0)
-            turn_x(u + 3, 1)
-            interleave_p(done, PACK * half, PACK * (half + 1))
+            newest = (u - 2) // HALVES
+            square_and_refill(u, 0)
+            turn_x(u + LOOKAHEAD, 0)
+            turn_x(u + LOOKAHEAD, 1)
+            interleave_p(u - 1)
+            if not odd:
+                take_log(newest - 1)
+            elif newest >= 2:
+                store_y(newest - 2)
+            square_and_refill(u, 1)
             if odd:
-                store_y(k - 2, True)
+                quantize_x(u + 2)
+                if newest >= 1:
+                    gain_and_bias(newest - 1)
+                if newest >= 2:
+                    quantize_y(newest - 2)
+                    store_codes(newest - 2, newest - 1)
             else:
-                take_log(k, (0, 1, 2, 3))
-            square(u, order[1])
-            filter_pass(u + 1, order[1])
+                if newest >= 2:
+                    round_y(newest - 2)
+                quantize_p(newest)
+                quantize_x(u + 2)
+            square_and_refill(u, 2)
             if odd:
-                quantize_x(ahead, PACK * part, PACK * (part + 1))
-                gain_and_bias(k - 1)
-                quantize_y(k - 2)
-                store_codes(k - 2, k - 1)
-            else:
-                round_y(k - 1)
-                quantize_p(done)
-                quantize_x(ahead, PACK * part, PACK * (part + 1))
-            square(u, order[2])
-            filter_pass(u + 1, order[2])
-            if odd:
-                average(k)
-            else:
-                turn_y(k - 1)
-            copy_x(u + 3, 0, True)
-            if u in ():
-                copy_x(u + 3, 1, True)
-            square(u, order[3])
-            filter_pass(u + 1, order[3])
-            if u not in ():
-                copy_x(u + 3, 1, False)
+                average(newest)
+            elif newest >= 2:
+                turn_y(newest - 2)
+            copy_x(u + LOOKAHEAD, 0, True)
+            square_and_refill(u, 3)
+            copy_x(u + LOOKAHEAD, 1, False)
 
         i = B - 1
         average(i - 1)
-        interleave_p(i, 0, 4)
+        interleave_p(last - 1)
         for j in range(PACK):
-            square(last, j, 0, 2)
+            square(last, j, 0, PAIR)
         gain_and_bias(i - 2)
-        turn_y(i - 2, 0, 4, "x_bank_0")
-        quantize_p(i, 0, 4)
+        turn_y(i - 2, tag="x_bank_0")
+        quantize_p(i, 0, PACK)
         for j in range(PACK):
-            square(last, j, 2, 4)
+            square(last, j, PAIR, PACK)
         for s in range(PACK):
-            open_average(i, s, "s_bank_%d" % s)
-        interleave_p(i, 4, 6)
-        take_log(i - 1, (0, 1, 2, 3))
-        interleave_p(i, 6, 8)
-        quantize_p(i, 4, 6)
-        average_pass(i, 0, 1)
-        average_pass(i, 1, 1)
-        quantize_p(i, 6, 8)
-        average_pass(i, 2, 1)
-        average_pass(i, 3, 1)
+            open_bank = psum.tile([P, R], F32, name="open_bank", tag="s_bank_%d" % s)
+            l_sums[i, s] = open_bank[:]
+            average_pass(i, s, 0)
+        interleave_p(last, 0, PAIR)
+        take_log(i - 1)
+        interleave_p(last, PAIR, PACK)
+        for s0 in (0, PAIR):
+            quantize_p(i, PACK + s0, PACK + s0 + PAIR)
+            average_pass(i, s0, 1)
+            average_pass(i, s0 + 1, 1)
         store_y(i - 3)
         store_y(i - 2)
         gain_and_bias(i - 1)
-        turn_y(i - 1, 0, 4, "x_bank_1")
-        take_log(i, (1, 0))
-        take_log(i, (3, 2))
+        turn_y(i - 1, tag="x_bank_1")
+        for s0 in (0, PAIR):
+            take_log(i, (s0 + 1, s0))
         quantize_y(i - 3)
         store_codes(i - 3, i - 2)
         round_y(i - 2)
-        gain_and_bias(i, 0, 2)
-        turn_y(i, 0, 2, "l_bank")
-        gain_and_bias(i, 2, 4)
-        turn_y(i, 2, 4)
-        store_y(i - 1, True)
+        for s0 in (0, PAIR):
+            gain_and_bias(i, s0, s0 + PAIR)
+            turn_y(i, s0, s0 + PAIR, "l_bank")
+        store_y(i - 1)
         round_y(i - 1)
         quantize_y(i - 2)
         round_y(i)

from contextlib import ExitStack

import concourse.mybir as mybir
from concourse.masks import make_identity

B, T, C, F, R = 8, 1024, 512, 512, 128
FLOPS = 2 * B * T * C * F + 2 * B * R * T * F

F32 = mybir.dt.float32
BF16 = mybir.dt.bfloat16
I32 = mybir.dt.int32
U32 = mybir.dt.uint32
U8 = mybir.dt.uint8
FP8X4 = mybir.dt.float8_e4m3fn_x4
ALU = mybir.AluOpType
ACT = mybir.ActivationFunctionType

P = 128
PACK = 4
SPAN = P * PACK
HALVES = T // SPAN
UNITS = B * HALVES
PAIR = 2
WORDS = SPAN // 2
RUN = 4
PADDED = 16
SQRT_FLOOR = 2.0 ** -116
LOOKAHEAD = 3
RAMP = 3
WARM_FIRST, WARM_SECOND = 7, 4
SLACK_BUFS = 4


def interleave_views(dst, src):
    return (
        dst.rearrange("p (c i j) -> p c j i", i=RUN, j=PACK),
        src.rearrange("p j (c i) -> p c j i", i=RUN),
    )


def tile_motor_imagery_log_power_h3_kernel(
    tc, x, filters, sample_weights, averaging, power_offset, gain, bias, out_0, out_1, out_2
):
    nc = tc.nc
    with ExitStack() as ctx:
        keep = ctx.enter_context(tc.tile_pool(name="keep", bufs=1))
        work = ctx.enter_context(tc.tile_pool(name="work", bufs=3))
        psum = ctx.enter_context(tc.psum_pool(name="psum", bufs=1))
        ctx.enter_context(tc.manual_schedule())

        x_rows = x.rearrange("b (g p j) c -> (b g) p j c", g=HALVES, j=PACK)
        x_raw, f_raw = {}, {}

        def load_x(u, h):
            x_raw[u, h] = keep.tile([P, PAIR * C], BF16, name="x_raw_%d_%d" % (u, h))
            nc.sync.dma_start(
                out=x_raw[u, h][:].rearrange("p (j c) -> p j c", j=PAIR),
                in_=x_rows[u, :, PAIR * h : PAIR * (h + 1), :],
            )

        w_raw = keep.tile([P, HALVES, PADDED], BF16)
        w = w_raw[:, :, 0:PACK]
        nc.sync.dma_start(out=w, in_=sample_weights.rearrange("(g p j) -> p g j", g=HALVES, j=PACK))
        for h in range(2):
            f_raw[h] = keep.tile([P, PACK, F // 2], BF16, name="f_raw_%d" % h)
            nc.sync.dma_start(
                out=f_raw[h][:], in_=filters.rearrange("(p j) f -> p j f", j=PACK)[:, :, h * F // 2 : (h + 1) * F // 2]
            )
            load_x(0, h)
        for u in range(1, RAMP):
            load_x(u, 0)
            load_x(u, 1)
        a_raw = keep.tile([P, T], BF16)
        nc.sync.dma_start(out=a_raw[:], in_=averaging)
        load_x(RAMP, 0)
        load_x(RAMP, 1)
        offset_col = keep.tile([P, PACK], BF16)
        gain_col = keep.tile([P, PACK], BF16)
        bias_col = keep.tile([P, PACK], BF16)
        for col, vec in ((offset_col, power_offset), (gain_col, gain), (bias_col, bias)):
            nc.sync.dma_start(out=col[:], in_=vec.rearrange("(p s) -> p s", s=PACK))
        for u in range(RAMP + 1, UNITS):
            load_x(u, 0)
            load_x(u, 1)

        ident = keep.tile([P, P], F32)
        make_identity(nc, ident[:])

        def quantize(codes, scales, grouped):
            nc.vector.quantize_mx(out=codes.bitcast(FP8X4), scales=scales, in_=grouped)

        def mx_pass(out, l_codes, l_scales, r_codes, r_scales, start=True, stop=True):
            nc.tensor.matmul_mx(
                out=out,
                lhsT=l_codes.bitcast(FP8X4),
                lhsT_scale=l_scales,
                rhs=r_codes.bitcast(FP8X4),
                rhs_scale=r_scales,
                start=start,
                stop=stop,
            )

        def copy(on_scalar, dst, src):
            if on_scalar:
                nc.scalar.copy(out=dst, in_=src)
            else:
                nc.vector.tensor_copy(out=dst, in_=src)

        warm_in = keep.tile([P, PAIR * SPAN], BF16, align_bytes=64)
        warm_codes = keep.tile([P, PAIR * P], U32, align_bytes=64)
        warm_scales = keep.tile([P, PAIR * P], U8, align_bytes=64)
        one = keep.tile([P, 1], F32)
        nc.vector.memset(warm_in[:], 1.0)
        nc.vector.memset(one[:], 1.0)
        quantize(warm_codes[:], warm_scales[:], warm_in[:])

        def warm_up(passes):
            warm_bank = psum.tile([P, PAIR * P], F32, name="warm_bank", tag="s_bank_3")
            for repeat in range(passes):
                mx_pass(warm_bank[:], warm_codes[:, 0:P], warm_scales[:, 0:P], warm_codes[:], warm_scales[:])

        w_abs = keep.tile([P, HALVES, PACK], F32)
        guess = keep.tile([P, HALVES, PACK], F32)
        guess_inv = keep.tile([P, HALVES, PACK], F32)
        half_quot = keep.tile([P, HALVES, PACK], F32)
        root = keep.tile([P, HALVES, PACK], F32)
        w_ge = keep.tile([P, HALVES, PACK], F32)
        w_sign = keep.tile([P, HALVES, PACK], BF16)
        nc.vector.scalar_tensor_tensor(out=w_abs[:], in0=w, scalar=-1.0, in1=w, op0=ALU.mult, op1=ALU.max)
        nc.vector.tensor_scalar(out=w_ge[:], in0=w, scalar1=0.0, scalar2=2.0, op0=ALU.is_ge, op1=ALU.mult)
        nc.scalar.activation(out=guess[:], in_=w_abs[:], func=ACT.Sqrt, bias=SQRT_FLOOR)
        nc.vector.tensor_scalar(out=w_sign[:], in0=w_ge[:], scalar1=-1.0, scalar2=None, op0=ALU.add)
        table_warm = keep.tile([P, 1], F32)
        nc.scalar.activation(out=table_warm[:], in_=one[:], func=ACT.Ln)

        f_grouped = keep.tile([P, PACK * F], BF16, align_bytes=64)
        f_codes = keep.tile([P, F], U32, align_bytes=64)
        f_scales = keep.tile([P, F], U8, align_bytes=64)
        a_turned = keep.tile([P, T], BF16, align_bytes=64)
        a_signed = keep.tile([P, T], BF16, align_bytes=64)
        a_codes = keep.tile([P, HALVES * R], U32, align_bytes=64)
        a_scales = keep.tile([P, HALVES * R], U8, align_bytes=64)
        y_codes = keep.tile([P, B * R], U32, align_bytes=64)
        y_scales = keep.tile([P, B * R], U8, align_bytes=64)
        x_bank, x_grouped, x_codes, x_scales = {}, {}, {}, {}
        s_bank, p_rows, p_grouped, p_codes, p_scales = {}, {}, {}, {}, {}
        l_sums, log_power, y_rows, y_grouped, y_bank = {}, {}, {}, {}, {}

        def turn_words(bank, words):
            for part in range(2):
                for e in range(2):
                    nc.tensor.transpose(
                        bank[:, part, e, :], words[:, WORDS * part + e : WORDS * (part + 1) : 2], ident[:]
                    )

        def join_words(on_scalar, grouped, bank):
            dst = grouped.bitcast(F32).rearrange("p (part m e) -> p part m e", part=2, e=2)
            copy(on_scalar, dst, bank.rearrange("p part e m -> p part m e"))

        def interleave_filters(h):
            span = slice(h * P // 2, (h + 1) * P // 2)
            nc.vector.tensor_copy(
                out=f_grouped[:].rearrange("p (s m j) -> p m s j", s=PACK, j=PACK)[:, span],
                in_=f_raw[h][:].rearrange("p j (m s) -> p m s j", s=PACK),
            )

        def turn_x(u, h, tag=None):
            if u < UNITS:
                x_bank[u, h] = psum.tile([P, PAIR, 2, P], F32, name="x_bank", tag=tag or "x_bank_%d" % h)
                turn_words(x_bank[u, h], x_raw[u, h][:].bitcast(F32))

        def copy_x(u, h, on_scalar):
            if u < UNITS:
                i, g = divmod(u, HALVES)
                if i not in x_grouped:
                    x_grouped[i] = work.tile(
                        [P, T * PACK], BF16, name="x_grouped", tag="x_grouped", bufs=SLACK_BUFS, align_bytes=64
                    )
                first = SPAN * (PACK * g + PAIR * h)
                join_words(on_scalar, x_grouped[i][:, first : first + PAIR * SPAN], x_bank[u, h][:])

        def quantize_x(u, j0=0, j1=PACK):
            if u < UNITS:
                i, g = divmod(u, HALVES)
                if i not in x_codes:
                    x_codes[i] = work.tile([P, T], U32, name="x_codes", tag="x_codes", align_bytes=64)
                    x_scales[i] = work.tile([P, T], U8, name="x_scales", tag="x_scales", align_bytes=64)
                n0, n1 = PACK * g + j0, PACK * g + j1
                cols = slice(P * n0, P * n1)
                quantize(x_codes[i][:, cols], x_scales[i][:, cols], x_grouped[i][:, SPAN * n0 : SPAN * n1])

        def filter_pass(u, j):
            i, g = divmod(u, HALVES)
            s_bank[u, j] = psum.tile([P, F], F32, name="s_bank", tag="s_bank_%d" % j)
            cols = slice(SPAN * g + P * j, SPAN * g + P * (j + 1))
            mx_pass(s_bank[u, j][:], x_codes[i][:, cols], x_scales[i][:, cols], f_codes[:], f_scales[:])

        def square(u, j, s0=0, s1=PACK):
            i, g = divmod(u, HALVES)
            if i not in p_rows:
                p_rows[i] = work.tile([P, HALVES, PACK, F], BF16, name="p_rows", tag="p_rows", bufs=SLACK_BUFS)
            cols = slice(P * s0, P * s1)
            nc.scalar.activation(
                out=p_rows[i][:, g, j, cols], in_=s_bank[u, j][:, cols], func=ACT.Square, scale=root[:, g, j : j + 1]
            )

        def square_and_refill(u, j):
            square(u, j)
            filter_pass(u + 1, j)

        def interleave_p(u, s0=0, s1=PACK):
            i, g = divmod(u, HALVES)
            if i not in p_grouped:
                p_grouped[i] = work.tile(
                    [P, HALVES * PACK * F], BF16, name="p_grouped", tag="p_grouped", bufs=2, align_bytes=64
                )
            dst = p_grouped[i][:, SPAN * (PACK * g + s0) : SPAN * (PACK * g + s1)]
            dst, src = interleave_views(dst, p_rows[i][:, g, :, P * s0 : P * s1])
            nc.vector.tensor_copy(out=dst, in_=src)

        def quantize_p(i, n0=0, n1=HALVES * PACK):
            if i not in p_codes:
                p_codes[i] = work.tile([P, HALVES * F], U32, name="p_codes", tag="p_codes", align_bytes=64)
                p_scales[i] = work.tile([P, HALVES * F], U8, name="p_scales", tag="p_scales", align_bytes=64)
            cols = slice(P * n0, P * n1)
            quantize(p_codes[i][:, cols], p_scales[i][:, cols], p_grouped[i][:, SPAN * n0 : SPAN * n1])

        def average_pass(i, s, g):
            cols = slice(F * g + P * s, F * g + P * (s + 1))
            windows = slice(R * g, R * (g + 1))
            mx_pass(
                l_sums[i, s],
                p_codes[i][:, cols],
                p_scales[i][:, cols],
                a_codes[:, windows],
                a_scales[:, windows],
                start=(g == 0),
                stop=(g == HALVES - 1),
            )

        def average(i):
            l_bank = psum.tile([P, PACK, R], F32, name="l_bank", tag="l_bank")
            for s in range(PACK):
                l_sums[i, s] = l_bank[:, s, :]
                for g in range(HALVES):
                    average_pass(i, s, g)

        def take_log(i, slots=range(PACK)):
            if i not in log_power:
                log_power[i] = work.tile([P, PACK, R], F32, name="log_power", tag="log_power", bufs=SLACK_BUFS)
            for s in slots:
                nc.scalar.activation(
                    out=log_power[i][:, s, :], in_=l_sums[i, s], func=ACT.Ln, bias=offset_col[:, s : s + 1]
                )

        def gain_and_bias(i, s0=0, s1=PACK):
            if i not in y_rows:
                y_rows[i] = work.tile([P, PACK, R], F32, name="y_rows", tag="y_rows")
            for s in reversed(range(s0, s1)):
                nc.vector.tensor_scalar(
                    out=y_rows[i][:, s, :],
                    in0=log_power[i][:, s, :],
                    scalar1=gain_col[:, s : s + 1],
                    scalar2=bias_col[:, s : s + 1],
                    op0=ALU.mult,
                    op1=ALU.add,
                )

        def round_y(i):
            y_grouped[i] = work.tile([P, PACK * R], BF16, name="y_grouped", tag="y_grouped", align_bytes=64)
            dst, src = interleave_views(y_grouped[i][:], y_rows[i][:])
            nc.vector.tensor_copy(out=dst, in_=src)

        def quantize_y(i):
            cols = slice(R * i, R * (i + 1))
            quantize(y_codes[:, cols], y_scales[:, cols], y_grouped[i][:])

        def store_codes(i0, i1):
            cols = slice(R * i0, R * i1)
            nc.sync.dma_start(
                out=out_1[0].rearrange("p m j -> p (m j)").bitcast(I32)[:, cols], in_=y_codes[:, cols].bitcast(I32)
            )

        def store_scales():
            for quadrant in range(4):
                queue = nc.sync if quadrant < 2 else nc.scalar
                queue.dma_start(
                    out=out_2[0, 4 * quadrant : 4 * quadrant + 4, :].bitcast(I32),
                    in_=y_scales[32 * quadrant : 32 * quadrant + 4, :].bitcast(I32),
                )

        def turn_y(i, s0=0, s1=PACK, tag="y_bank"):
            if i not in y_bank:
                y_bank[i] = psum.tile([P, PACK, P], F32, name="y_bank", tag=tag)
            for s in range(s0, s1):
                nc.tensor.transpose(y_bank[i][:, s, :], y_rows[i][:, s, :], ident[:])

        def store_y(i):
            y_out = work.tile([P, F], F32, name="y_out", tag="y_out", bufs=B)
            nc.scalar.copy(
                out=y_out[:].rearrange("r (m s) -> r m s", s=PACK), in_=y_bank[i][:].rearrange("r s m -> r m s")
            )
            nc.sync.dma_start(out=out_0[i], in_=y_out[:])

        warm_up(WARM_FIRST)
        turn_x(0, 0)
        warm_up(WARM_SECOND)
        interleave_filters(0)
        nc.vector.reciprocal(out=guess_inv[:], in_=guess[:])
        interleave_filters(1)
        nc.vector.scalar_tensor_tensor(
            out=half_quot[:], in0=w_abs[:], scalar=0.5, in1=guess_inv[:], op0=ALU.mult, op1=ALU.mult
        )
        turn_x(0, 1)
        turn_x(1, 0, "l_bank")
        copy_x(0, 0, True)
        quantize(f_codes[:], f_scales[:], f_grouped[:])
        quantize_x(0, 0, PAIR)
        nc.vector.scalar_tensor_tensor(
            out=root[:], in0=guess[:], scalar=0.5, in1=half_quot[:], op0=ALU.mult, op1=ALU.add
        )
        copy_x(0, 1, True)
        filter_pass(0, 0)
        filter_pass(0, 1)
        turn_x(1, 1, "y_bank")
        copy_x(1, 0, False)
        quantize_x(0, PAIR, PACK)
        copy_x(1, 1, False)
        filter_pass(0, 2)
        filter_pass(0, 3)

        turn_x(2, 0)
        turn_x(2, 1)
        quantize_x(1)
        square_and_refill(0, 0)
        square_and_refill(0, 1)
        copy_x(2, 0, False)
        copy_x(2, 1, False)
        square_and_refill(0, 2)
        square_and_refill(0, 3)

        turn_x(3, 0)
        turn_x(3, 1)
        quantize_x(2)
        square_and_refill(1, 0)
        square_and_refill(1, 1)
        a_bank = psum.tile([P, HALVES, 2, R], F32, name="a_bank", tag="y_bank")
        turn_words(a_bank, a_raw[:].bitcast(F32))
        interleave_p(0)
        square_and_refill(1, 2)
        copy_x(3, 0, True)
        copy_x(3, 1, False)
        turn_x(4, 0)
        square_and_refill(1, 3)

        turn_x(4, 1)
        interleave_p(1)
        quantize_x(3)
        square_and_refill(2, 0)
        join_words(True, a_turned[:], a_bank[:])
        square_and_refill(2, 1)
        copy_x(4, 1, True)
        copy_x(4, 0, True)
        turn_x(5, 0)
        quantize_p(0)
        nc.vector.tensor_tensor(
            out=a_signed[:].rearrange("p (g r j) -> p g r j", g=HALVES, j=PACK),
            in0=a_turned[:].rearrange("p (g r j) -> p g r j", g=HALVES, j=PACK),
            in1=w_sign[:].unsqueeze(2).to_broadcast([P, HALVES, R, PACK]),
            op=ALU.mult,
        )
        square_and_refill(2, 2)
        turn_x(5, 1)
        quantize_x(4)
        square_and_refill(2, 3)
        quantize(a_codes[:], a_scales[:], a_signed[:])
        copy_x(5, 0, True)
        copy_x(5, 1, False)

        last = UNITS - 1
        for u in range(RAMP, last):
            odd = u % 2 == 1
            newest = (u - 2) // HALVES
            square_and_refill(u, 0)
            turn_x(u + LOOKAHEAD, 0)
            turn_x(u + LOOKAHEAD, 1)
            interleave_p(u - 1)
            if not odd:
                take_log(newest - 1)
            elif newest >= 2:
                store_y(newest - 2)
            square_and_refill(u, 1)
            if odd:
                quantize_x(u + 2)
                if newest >= 1:
                    gain_and_bias(newest - 1)
                if newest >= 2:
                    quantize_y(newest - 2)
                    store_codes(newest - 2, newest - 1)
            else:
                if newest >= 2:
                    round_y(newest - 2)
                quantize_p(newest)
                quantize_x(u + 2)
            square_and_refill(u, 2)
            if odd:
                average(newest)
            elif newest >= 2:
                turn_y(newest - 2)
            copy_x(u + LOOKAHEAD, 0, True)
            square_and_refill(u, 3)
            copy_x(u + LOOKAHEAD, 1, False)

        i = B - 1
        average(i - 1)
        interleave_p(last - 1)
        for j in range(PACK):
            square(last, j, 0, PAIR)
        gain_and_bias(i - 2)
        turn_y(i - 2, tag="x_bank_0")
        quantize_p(i, 0, PACK)
        for j in range(PACK):
            square(last, j, PAIR, PACK)
        for s in range(PACK):
            open_bank = psum.tile([P, R], F32, name="open_bank", tag="s_bank_%d" % s)
            l_sums[i, s] = open_bank[:]
            average_pass(i, s, 0)
        interleave_p(last, 0, PAIR)
        take_log(i - 1)
        interleave_p(last, PAIR, PACK)
        for s0 in (0, PAIR):
            quantize_p(i, PACK + s0, PACK + s0 + PAIR)
            average_pass(i, s0, 1)
            average_pass(i, s0 + 1, 1)
        store_y(i - 3)
        store_y(i - 2)
        gain_and_bias(i - 1)
        turn_y(i - 1, tag="x_bank_1")
        for s0 in (0, PAIR):
            take_log(i, (s0 + 1, s0))
        quantize_y(i - 3)
        store_codes(i - 3, i - 2)
        round_y(i - 2)
        for s0 in (0, PAIR):
            gain_and_bias(i, s0, s0 + PAIR)
            turn_y(i, s0, s0 + PAIR, "l_bank")
        store_y(i - 1)
        round_y(i - 1)
        quantize_y(i - 2)
        round_y(i)
        quantize_y(i - 1)
        store_y(i)
        quantize_y(i)
        store_codes(i - 2, B)
        store_scales()
